import numpy as np
import ml_dtypes


def mxq(x, axis, fmt="e4m3"):
    dtype, down = {"e4m3": (ml_dtypes.float8_e4m3fn, 7), "e5m2": (ml_dtypes.float8_e5m2, 14)}[fmt]
    v = np.moveaxis(np.asarray(x, np.float32).astype(ml_dtypes.bfloat16).astype(np.float64), axis, -1)
    blocks = v.reshape(v.shape[:-1] + (-1, 32))
    amax = np.abs(blocks).max(-1, keepdims=True)
    byte = np.maximum(np.where(amax > 0, np.frexp(amax)[1] - 1 + 127, 0) - down, 1)
    scale = np.exp2(byte - 127.0)
    codes = (blocks / scale).astype(np.float32).astype(dtype).astype(np.float64)
    return np.moveaxis((codes * scale).reshape(v.shape), -1, axis)


WIDE = False


def mx_kscale(k):
    if not WIDE:
        return np.ones(k)
    levels = np.array([24, -24, 12, -12, 0])
    if k % 512:
        return np.exp2(np.random.permutation(np.resize(levels, k // 32))).repeat(32)
    a = np.empty((k // 512, 16))
    for p in range(k // 512):
        a[p, :8] = np.random.permutation(np.resize(levels, 8))
        for g in range(8):
            far = levels[np.abs(levels - a[p, g]) >= 10]
            a[p, g + 8] = far[np.random.randint(len(far))]
    return np.exp2(a.ravel()).repeat(32)


def f64(x):
    return np.asarray(x).astype(np.float64)


def striped(idx):
    return np.tile(idx.reshape(-1, 16).T, (8, 1)).astype(np.uint16)


def unstriped(offs):
    return offs[:16].T.reshape(-1).astype(np.int64)


E2M1 = np.array([0.0, 0.5, 1.0, 1.5, 2.0, 3.0, 4.0, 6.0, -0.0, -0.5, -1.0, -1.5, -2.0, -3.0, -4.0, -6.0])


def pack_weight(w, fmt):
    k, n = w.shape
    w = f64(np.asarray(w, np.float32).astype(ml_dtypes.bfloat16)).reshape(k // 32, 32, n)
    amax = np.abs(w).max(1)
    if fmt == "e4m3":
        byte = np.frexp(amax)[1] - 1 + 127 - 7
    else:
        mant, ex = np.frexp(amax / 6.0)
        byte = np.where(mant > 0.5, ex, ex - 1) + 127
    byte = np.clip(np.where(amax > 0, byte, 1), 1, 254)
    scaled = (w * np.exp2(127.0 - byte)[:, None, :]).reshape(k, n).astype(np.float32)
    by_word = np.ascontiguousarray(scaled.reshape(k // 512, 128, 4, n).transpose(0, 1, 3, 2))
    if fmt == "e4m3":
        words = by_word.astype(ml_dtypes.float8_e4m3fn).view(np.uint8)
    else:
        c = by_word.astype(ml_dtypes.float4_e2m1fn).view(np.uint8) & 0xF
        words = (c[..., 0::2] | (c[..., 1::2] << 4)).reshape(k // 512, 128, 2 * n)
    return np.ascontiguousarray(words), np.ascontiguousarray(byte.astype(np.uint8).reshape(k // 512, 16, n))


def unpack_weight(words, scales, fmt):
    g, _, n = scales.shape
    words = np.ascontiguousarray(words).reshape(g, 128, n, -1)
    if fmt == "e4m3":
        vals = words.view(ml_dtypes.float8_e4m3fn).astype(np.float64)
    else:
        nib = np.empty((g, 128, n, 4), np.uint8)
        nib[..., 0::2] = words & 0xF
        nib[..., 1::2] = words >> 4
        vals = E2M1[nib]
    vals = vals * np.repeat(np.exp2(scales.astype(np.float64) - 127.0), 8, axis=1)[..., None]
    return vals.transpose(0, 1, 3, 2).reshape(g * 512, n)


def gelu(f):
    return 0.5 * f * (1.0 + np.tanh(np.sqrt(2.0 / np.pi) * (f + 0.044715 * f**3)))


K, R, N, T, J = 512, 1024, 256, 4096, 1024


def setup_inputs():
    n = np.random.standard_normal
    s = mx_kscale(K)[:, None]
    u = mx_kscale(R)[:, None]
    p_tab = pack_weight(n((K, T)) * s, "e4m3")
    p_w0 = pack_weight(n((K, R)) / np.sqrt(3 * K) / s, "e2m1")
    p_w1 = pack_weight(n((K, R)) / np.sqrt(3 * K) / s, "e2m1")
    p_w2 = pack_weight(n((K, R)) / np.sqrt(3 * K) / s, "e2m1")
    return {
        "tab_words": p_tab[0],
        "tab_scales": p_tab[1],
        "w0_words": p_w0[0],
        "w0_scales": p_w0[1],
        "w1_words": p_w1[0],
        "w1_scales": p_w1[1],
        "w2_words": p_w2[0],
        "w2_scales": p_w2[1],
        "sm": (np.random.uniform(0.5, 2.0, R) * u[:, 0]).astype(np.float32),
        "wd": (n((R, N)) / np.sqrt(R) / u).astype(np.float32),
        "b": (0.3 * n(N)).astype(np.float32),
        "offs": striped(np.concatenate([np.random.permutation(T)[:J] for _ in range(3)])),
    }


def reference(tab_words, tab_scales, w0_words, w0_scales, w1_words, w1_scales, w2_words, w2_scales, sm, wd, b, offs):
    idx = unstriped(offs).reshape(3, J)
    tab_ = unpack_weight(tab_words, tab_scales, "e4m3")[:, idx]
    w0_ = unpack_weight(w0_words, w0_scales, "e2m1")
    w1_ = unpack_weight(w1_words, w1_scales, "e2m1")
    w2_ = unpack_weight(w2_words, w2_scales, "e2m1")
    a = w0_.T @ tab_[:, 0] + w1_.T @ tab_[:, 1] + w2_.T @ tab_[:, 2]
    h = f64(sm)[:, None] * gelu(a)
    h_ = mxq(h, 0, "e4m3")
    wd_ = mxq(f64(wd), 0, "e4m3")
    y = wd_.T @ h_
    return gelu(y + f64(b)[:, None])

@@ -1,0 +1,214 @@
+from contextlib import ExitStack
+
+import concourse.mybir as mybir
+from concourse.masks import make_identity
+
+K, R, N, T, J = 512, 1024, 256, 4096, 1024
+LISTS = 3
+FLOPS = 2 * LISTS * K * R * J + 2 * R * N * J
+
+F32 = mybir.dt.float32
+BF16 = mybir.dt.bfloat16
+I32 = mybir.dt.int32
+U32 = mybir.dt.uint32
+U16 = mybir.dt.uint16
+U8 = mybir.dt.uint8
+FP8X4 = mybir.dt.float8_e4m3fn_x4
+FP4X4 = mybir.dt.float4_e2m1fn_x4
+GELU = mybir.ActivationFunctionType.Gelu_apprx_tanh
+COPY = mybir.ActivationFunctionType.Copy
+MULT = mybir.AluOpType.mult
+
+P = 128
+PACK = 4
+PASSES = R // (P * PACK)
+SLOTS = PASSES * PACK
+CHUNK = 512
+PIECE = 256
+
+
+def tile_list_rvq_gelu_gelu_kernel(
+    tc, tab_words, tab_scales, w0_words, w0_scales, w1_words, w1_scales, w2_words, w2_scales, sm, wd, b, offs, out
+):
+    nc = tc.nc
+    w_words = (w0_words, w1_words, w2_words)
+    w_scales = (w0_scales, w1_scales, w2_scales)
+    chunks = J // CHUNK
+
+    with ExitStack() as ctx:
+        keep = ctx.enter_context(tc.tile_pool(name="keep", bufs=1))
+        psum = ctx.enter_context(tc.psum_pool(name="psum", bufs=1))
+
+        offsets = keep.tile([P, LISTS * J // 16], U16, name="offsets")
+        table = keep.tile([P, T], I32, name="table", align_bytes=64)
+        table_sc = keep.tile([P, T // 4], I32, name="table_sc", tag="table_sc", align_bytes=64)
+        nc.gpsimd.memset(table_sc[:, 0 : 5 * T // 32], 0)
+        nc.vector.memset(table_sc[:, 5 * T // 32 : T // 4], 0)
+        nc.sync.dma_start(offsets[:], offs)
+        nc.sync.dma_start(table_sc[0:P:8, :], tab_scales[0].bitcast(I32))
+        w_sc = keep.tile([P, LISTS * R // 4], I32, name="w_sc", align_bytes=64)
+        sc_raw = keep.tile([16, LISTS, R // 4], I32, name="sc_raw", align_bytes=64)
+        for g in range(LISTS):
+            nc.sync.dma_start(sc_raw[:, g, :], w_scales[g][0].bitcast(I32))
+
+        def load_words(g):
+            raw = keep.tile([P, R // 2], I32, name=f"w_raw{g}", tag=f"stage{min(g, 1)}", align_bytes=64)
+            nc.sync.dma_start(raw[:], w_words[g][0].bitcast(I32))
+            return raw
+
+        w_raw = [load_words(0), load_words(1)]
+        nc.sync.dma_start(table[:], tab_words[0].rearrange("p t i -> p (t i)").bitcast(I32))
+        nc.vector.tensor_copy(
+            w_sc[0:16, :].rearrange("p (g s q x) -> p g s q x", g=LISTS, s=SLOTS, x=2),
+            sc_raw[:].rearrange("p g (q s x) -> p g s q x", s=SLOTS, x=2),
+        )
+        for quad in range(1, 4):
+            nc.scalar.dma_start(w_sc[32 * quad : 32 * quad + 4, :], w_sc[4 * quad : 4 * quad + 4, :])
+
+        ident = keep.tile([P, P], F32, name="ident")
+        make_identity(nc, ident[:])
+        planes = []
+        for c in range(chunks):
+            plane = keep.tile([P, LISTS * CHUNK // 4], I32, name=f"plane{c}", align_bytes=64)
+            planes.append(plane)
+
+        def list_slice(c, g):
+            first = (g * J + c * CHUNK) // 16
+            return offsets[:, first : first + CHUNK // 16]
+
+        def gather_scales(c):
+            picked = keep.tile([P, LISTS * CHUNK], U8, name=f"picked_sc{c}", tag=("picked_sc", "stage1")[c], align_bytes=64)
+            for g in range(LISTS):
+                nc.vector.tensor_copy(
+                    picked[:, g * CHUNK : (g + 1) * CHUNK], table_sc[:].bitcast(U8).indirect(list_slice(c, g))
+                )
+            for quad in range(4):
+                (nc.scalar, nc.sync)[c].dma_start(
+                    planes[c][32 * quad : 32 * quad + 4, :], picked[:].bitcast(I32)[32 * quad : 32 * quad + 32 : 8, :]
+                )
+
+        def gather_words(c, g, picked):
+            nc.vector.tensor_copy(picked[:, g, :], table[:].bitcast(U32).indirect(list_slice(c, g)))
+            return picked[:, g, :]
+
+        def order_words(g):
+            ordered = keep.tile([P, R // 2], I32, name=f"w_ord{g}", align_bytes=64)
+            nc.vector.tensor_copy(
+                ordered[:].rearrange("p (s q x) -> p s q x", s=SLOTS, x=4),
+                w_raw[g][:].rearrange("p (q s x) -> p s q x", s=SLOTS, x=4),
+            )
+            return ordered
+
+        gather_scales(0)
+        w_ord = []
+        picked_words = {}
+        picked0 = keep.tile([P, LISTS, CHUNK], U32, name="picked0", align_bytes=64)
+        for g in range(LISTS):
+            if g == 2:
+                w_raw.append(load_words(2))
+            w_ord.append(order_words(g))
+            picked_words[0, g] = gather_words(0, g, picked0)
+        rows = keep.tile([P, P], F32, name="rows", tag="stage0", align_bytes=64)
+        nc.gpsimd.memset(rows[:], 0.0)
+        nc.sync.dma_start(
+            rows[0:SLOTS, :].rearrange("s (q i) -> s q i", i=8), sm.rearrange("(q s i) -> s q i", s=SLOTS, i=8)
+        )
+        nc.sync.dma_start(rows[SLOTS : SLOTS + N // P, :], b.rearrange("(c p) -> c p", p=P))
+        turned = psum.tile([P, P], F32, name="turned", tag="bank7")
+        nc.tensor.transpose(turned[:], rows[:], ident[:])
+        cols = keep.tile([P, 16], F32, name="cols")
+        nc.scalar.copy(cols[:], turned[:, 0:16])
+
+        gather_scales(1)
+        picked1 = keep.tile([P, LISTS, CHUNK], U32, name="picked1", tag="table_sc", align_bytes=64)
+        for g in range(LISTS):
+            picked_words[1, g] = gather_words(1, g, picked1)
+
+        wd_raw = keep.tile([P, SLOTS, N], F32, name="wd_raw", tag="picked_sc", align_bytes=64)
+        wd_rows = wd.rearrange("(q s i) n -> i q s n", s=SLOTS, i=8)
+        for i in range(8):
+            nc.sync.dma_start(wd_raw[i:P:8, :, :], wd_rows[i])
+
+        wd_bf = keep.tile([P, PASSES, N, PACK], BF16, name="wd_bf", align_bytes=64)
+        for a in range(PASSES):
+            nc.scalar.activation(
+                wd_bf[:, a].rearrange("p (c e) t -> p c t e", e=2),
+                wd_raw[:, a * PACK : (a + 1) * PACK, :].rearrange("p t (c e) -> p c t e", e=2),
+                COPY,
+            )
+        wd_codes = keep.tile([P, PASSES * N], U32, name="wd_codes", align_bytes=64)
+        wd_sc = keep.tile([P, PASSES * N], U8, name="wd_sc", align_bytes=64)
+        nc.vector.quantize_mx(
+            out=wd_codes[:].bitcast(FP8X4), scales=wd_sc[:], in_=wd_bf[:].rearrange("p a n t -> p (a n t)")
+        )
+
+        all_acts = []
+        for c in range(chunks):
+            act = keep.tile([P, SLOTS, CHUNK], F32, name=f"act{c}", tag=("act", "picked_sc")[c], align_bytes=64)
+            acts = [act[:, a * PACK : (a + 1) * PACK, :] for a in range(PASSES)]
+            all_acts.append(acts)
+            accs = []
+            for s in range(SLOTS):
+                acc = psum.tile([P, CHUNK], F32, name=f"acc{c}_{s}", tag=f"bank{s}")
+                accs.append(acc)
+            steps = [(s, g) for g in range(LISTS) for s in range(PACK)]
+            steps.extend([(s, g) for s in range(PACK, SLOTS) for g in range(LISTS)])
+            for s, g in steps:
+                nc.tensor.matmul_mx(
+                    out=accs[s][:],
+                    lhsT=w_ord[g][:].bitcast(U8)[:, 2 * P * s : 2 * P * (s + 1)].bitcast(FP4X4),
+                    lhsT_scale=w_sc[:].bitcast(U8)[:, g * R + P * s : g * R + P * (s + 1)],
+                    rhs=picked_words[c, g].bitcast(FP8X4),
+                    rhs_scale=planes[c][:].bitcast(U8)[:, g * CHUNK : (g + 1) * CHUNK],
+                    start=(g == 0),
+                    stop=(g == LISTS - 1),
+                )
+                if g == LISTS - 1:
+                    nc.scalar.activation(acts[s // PACK][:, s % PACK, :], accs[s][:], GELU)
+
+        for c in range(chunks):
+            acts = all_acts[c]
+            for h in range(CHUNK // PIECE):
+                js = slice(h * PIECE, (h + 1) * PIECE)
+                u = c * (CHUNK // PIECE) + h
+                h_codes = []
+                h_scs = []
+                h_bfs = []
+                for a in range(PASSES):
+                    h_bf = keep.tile([P, PIECE, PACK], BF16, name=f"h_bf{u}_{a}", align_bytes=64)
+                    factor = cols[:, a * PACK : (a + 1) * PACK].unsqueeze(1).unsqueeze(3)
+                    nc.vector.tensor_tensor(
+                        h_bf[:].rearrange("p (c e) t -> p c t e", e=2),
+                        acts[a][:, :, js].rearrange("p t (c e) -> p c t e", e=2),
+                        factor.to_broadcast([P, PIECE // 2, PACK, 2]),
+                        MULT,
+                    )
+                    h_bfs.append(h_bf)
+                for a in range(PASSES):
+                    codes = keep.tile([P, PIECE], U32, name=f"h_codes{u}_{a}", align_bytes=64)
+                    h_sc = keep.tile([P, PIECE], U8, name=f"h_sc{u}_{a}", align_bytes=64)
+                    nc.vector.quantize_mx(
+                        out=codes[:].bitcast(FP8X4), scales=h_sc[:], in_=h_bfs[a][:].rearrange("p j t -> p (j t)")
+                    )
+                    h_codes.append(codes)
+                    h_scs.append(h_sc)
+                ybank = psum.tile([P, N // P, PIECE], F32, name=f"y{u}", tag=f"bank{6 + u % 2}")
+                result = keep.tile([P, N // P, PIECE], F32, name=f"result{u}")
+                for m in range(N // P):
+                    for a in range(PASSES):
+                        first = a * N + m * P
+                        nc.tensor.matmul_mx(
+                            out=ybank[:, m, :],
+                            lhsT=wd_codes[:, first : first + P].bitcast(FP8X4),
+                            lhsT_scale=wd_sc[:, first : first + P],
+                            rhs=h_codes[a][:].bitcast(FP8X4),
+                            rhs_scale=h_scs[a][:],
+                            start=(a == 0),
+                            stop=(a == PASSES - 1),
+                        )
+                for m in range(N // P):
+                    nc.scalar.activation(
+                        result[:, m, :], ybank[:, m, :], GELU, bias=cols[:, SLOTS + m : SLOTS + m + 1]
+                    )
+                j0 = c * CHUNK + h * PIECE
+                nc.sync.dma_start(out[:, j0 : j0 + PIECE].rearrange("(m p) j -> p m j", p=P), result[:])

@@ -18,6 +18,7 @@ FP4X4 = mybir.dt.float4_e2m1fn_x4
 GELU = mybir.ActivationFunctionType.Gelu_apprx_tanh
 COPY = mybir.ActivationFunctionType.Copy
 MULT = mybir.AluOpType.mult
+ADD = mybir.AluOpType.add
 
 P = 128
 PACK = 4
@@ -50,21 +51,18 @@ def tile_list_rvq_gelu_gelu_kernel(
         sc_raw = keep.tile([16, LISTS, R // 4], I32, name="sc_raw", align_bytes=64)
         for g in range(LISTS):
             nc.sync.dma_start(sc_raw[:, g, :], w_scales[g][0].bitcast(I32))
-
-        def load_words(g):
-            raw = keep.tile([P, R // 2], I32, name=f"w_raw{g}", tag=f"stage{min(g, 1)}", align_bytes=64)
+        w_raw = []
+        for g in range(LISTS):
+            raw = keep.tile([P, R // 2], I32, name=f"w_raw{g}", tag=f"stage{g}", align_bytes=64)
             nc.sync.dma_start(raw[:], w_words[g][0].bitcast(I32))
-            return raw
-
-        w_raw = [load_words(0), load_words(1)]
+            w_raw.append(raw)
         nc.sync.dma_start(table[:], tab_words[0].rearrange("p t i -> p (t i)").bitcast(I32))
         nc.vector.tensor_copy(
             w_sc[0:16, :].rearrange("p (g s q x) -> p g s q x", g=LISTS, s=SLOTS, x=2),
             sc_raw[:].rearrange("p g (q s x) -> p g s q x", s=SLOTS, x=2),
         )
         for quad in range(1, 4):
-            nc.scalar.dma_start(w_sc[32 * quad : 32 * quad + 4, :], w_sc[4 * quad : 4 * quad + 4, :])
-
+            nc.sync.dma_start(w_sc[32 * quad : 32 * quad + 4, :], w_sc[4 * quad : 4 * quad + 4, :])
         ident = keep.tile([P, P], F32, name="ident")
         make_identity(nc, ident[:])
         planes = []
@@ -77,13 +75,13 @@ def tile_list_rvq_gelu_gelu_kernel(
             return offsets[:, first : first + CHUNK // 16]
 
         def gather_scales(c):
-            picked = keep.tile([P, LISTS * CHUNK], U8, name=f"picked_sc{c}", tag=("picked_sc", "stage1")[c], align_bytes=64)
+            picked = keep.tile([P, LISTS * CHUNK], U8, name=f"picked_sc{c}", tag=("picked_sc", "stage0")[c], align_bytes=64)
             for g in range(LISTS):
                 nc.vector.tensor_copy(
                     picked[:, g * CHUNK : (g + 1) * CHUNK], table_sc[:].bitcast(U8).indirect(list_slice(c, g))
                 )
             for quad in range(4):
-                (nc.scalar, nc.sync)[c].dma_start(
+                nc.sync.dma_start(
                     planes[c][32 * quad : 32 * quad + 4, :], picked[:].bitcast(I32)[32 * quad : 32 * quad + 32 : 8, :]
                 )
 
@@ -100,13 +98,10 @@ def tile_list_rvq_gelu_gelu_kernel(
             return ordered
 
         gather_scales(0)
-        w_ord = []
+        w_ord = [order_words(g) for g in range(LISTS)]
         picked_words = {}
         picked0 = keep.tile([P, LISTS, CHUNK], U32, name="picked0", align_bytes=64)
         for g in range(LISTS):
-            if g == 2:
-                w_raw.append(load_words(2))
-            w_ord.append(order_words(g))
             picked_words[0, g] = gather_words(0, g, picked0)
         rows = keep.tile([P, P], F32, name="rows", tag="stage0", align_bytes=64)
         nc.gpsimd.memset(rows[:], 0.0)
@@ -119,40 +114,31 @@ def tile_list_rvq_gelu_gelu_kernel(
         cols = keep.tile([P, 16], F32, name="cols")
         nc.scalar.copy(cols[:], turned[:, 0:16])
 
+        wd_raw = keep.tile([P, SLOTS, N], F32, name="wd_raw", tag="stage2", align_bytes=64)
+        wd_rows = wd.rearrange("(q s i) n -> i q s n", s=SLOTS, i=8)
+        for i in range(8):
+            nc.sync.dma_start(wd_raw[i:P:8, :, :], wd_rows[i])
+
         gather_scales(1)
         picked1 = keep.tile([P, LISTS, CHUNK], U32, name="picked1", tag="table_sc", align_bytes=64)
         for g in range(LISTS):
             picked_words[1, g] = gather_words(1, g, picked1)
 
-        wd_raw = keep.tile([P, SLOTS, N], F32, name="wd_raw", tag="picked_sc", align_bytes=64)
-        wd_rows = wd.rearrange("(q s i) n -> i q s n", s=SLOTS, i=8)
-        for i in range(8):
-            nc.sync.dma_start(wd_raw[i:P:8, :, :], wd_rows[i])
-
-        wd_bf = keep.tile([P, PASSES, N, PACK], BF16, name="wd_bf", align_bytes=64)
-        for a in range(PASSES):
-            nc.scalar.activation(
-                wd_bf[:, a].rearrange("p (c e) t -> p c t e", e=2),
-                wd_raw[:, a * PACK : (a + 1) * PACK, :].rearrange("p t (c e) -> p c t e", e=2),
-                COPY,
-            )
-        wd_codes = keep.tile([P, PASSES * N], U32, name="wd_codes", align_bytes=64)
-        wd_sc = keep.tile([P, PASSES * N], U8, name="wd_sc", align_bytes=64)
-        nc.vector.quantize_mx(
-            out=wd_codes[:].bitcast(FP8X4), scales=wd_sc[:], in_=wd_bf[:].rearrange("p a n t -> p (a n t)")
-        )
-
         all_acts = []
         for c in range(chunks):
-            act = keep.tile([P, SLOTS, CHUNK], F32, name=f"act{c}", tag=("act", "picked_sc")[c], align_bytes=64)
-            acts = [act[:, a * PACK : (a + 1) * PACK, :] for a in range(PASSES)]
+            acts = []
+            for a in range(PASSES):
+                tag = "wd_bf" if (c, a) == (0, 0) else f"act{c}_{a}"
+                act = keep.tile([P, PACK, CHUNK], F32, name=f"act{c}_{a}", tag=tag, align_bytes=64)
+                acts.append(act)
             all_acts.append(acts)
             accs = []
             for s in range(SLOTS):
                 acc = psum.tile([P, CHUNK], F32, name=f"acc{c}_{s}", tag=f"bank{s}")
                 accs.append(acc)
-            steps = [(s, g) for g in range(LISTS) for s in range(PACK)]
-            steps.extend([(s, g) for s in range(PACK, SLOTS) for g in range(LISTS)])
+            ahead = (2, 4)[c]
+            steps = [(s, g) for g in range(LISTS) for s in range(ahead)]
+            steps.extend([(s, g) for s in range(ahead, SLOTS) for g in range(LISTS)])
             for s, g in steps:
                 nc.tensor.matmul_mx(
                     out=accs[s][:],
@@ -165,9 +151,34 @@ def tile_list_rvq_gelu_gelu_kernel(
                 )
                 if g == LISTS - 1:
                     nc.scalar.activation(acts[s // PACK][:, s % PACK, :], accs[s][:], GELU)
+            if c == 0:
+                scaled = keep.tile([P, PACK, CHUNK], BF16, name="scaled", align_bytes=64)
+                woven = keep.tile([P, CHUNK, PACK], BF16, name="woven", align_bytes=64)
+                for t in range(PACK):
+                    nc.gpsimd.tensor_scalar(scaled[:, t, :], acts[0][:, t, :], cols[:, t : t + 1], 0.0, MULT, ADD)
+                for h in range(CHUNK // PIECE):
+                    js = slice(h * PIECE, (h + 1) * PIECE)
+                    nc.scalar.copy(
+                        woven[:, js, :].rearrange("p (c e) t -> p c t e", e=4),
+                        scaled[:, :, js].rearrange("p t (c e) -> p c t e", e=4),
+                    )
+
+        wd_bf = keep.tile([P, PASSES, N, PACK], BF16, name="wd_bf", tag="wd_bf", align_bytes=64)
+        for a in range(PASSES):
+            nc.gpsimd.tensor_scalar(
+                wd_bf[:, a], wd_raw[:, a * PACK : (a + 1) * PACK, :].rearrange("p t n -> p n t"), 1.0, 0.0, MULT, ADD
+            )
+        wd_codes = keep.tile([P, PASSES * N], U32, name="wd_codes", align_bytes=64)
+        wd_sc = keep.tile([P, PASSES * N], U8, name="wd_sc", align_bytes=64)
+        nc.vector.quantize_mx(
+            out=wd_codes[:].bitcast(FP8X4), scales=wd_sc[:], in_=wd_bf[:].rearrange("p a n t -> p (a n t)")
+        )
 
         for c in range(chunks):
             acts = all_acts[c]
+            h_all = keep.tile(
+                [P, PASSES, CHUNK, PACK], BF16, name=f"h_all{c}", tag=("h_all", "wd_bf")[c], align_bytes=64
+            )
             for h in range(CHUNK // PIECE):
                 js = slice(h * PIECE, (h + 1) * PIECE)
                 u = c * (CHUNK // PIECE) + h
@@ -175,10 +186,13 @@ def tile_list_rvq_gelu_gelu_kernel(
                 h_scs = []
                 h_bfs = []
                 for a in range(PASSES):
-                    h_bf = keep.tile([P, PIECE, PACK], BF16, name=f"h_bf{u}_{a}", align_bytes=64)
+                    if (c, a) == (0, 0):
+                        h_bfs.append(woven[:, js, :])
+                        continue
+                    h_bf = h_all[:, a, js, :]
                     factor = cols[:, a * PACK : (a + 1) * PACK].unsqueeze(1).unsqueeze(3)
                     nc.vector.tensor_tensor(
-                        h_bf[:].rearrange("p (c e) t -> p c t e", e=2),
+                        h_bf.rearrange("p (c e) t -> p c t e", e=2),
                         acts[a][:, :, js].rearrange("p t (c e) -> p c t e", e=2),
                         factor.to_broadcast([P, PIECE // 2, PACK, 2]),
                         MULT,
@@ -188,7 +202,7 @@ def tile_list_rvq_gelu_gelu_kernel(
                     codes = keep.tile([P, PIECE], U32, name=f"h_codes{u}_{a}", align_bytes=64)
                     h_sc = keep.tile([P, PIECE], U8, name=f"h_sc{u}_{a}", align_bytes=64)
                     nc.vector.quantize_mx(
-                        out=codes[:].bitcast(FP8X4), scales=h_sc[:], in_=h_bfs[a][:].rearrange("p j t -> p (j t)")
+                        out=codes[:].bitcast(FP8X4), scales=h_sc[:], in_=h_bfs[a].rearrange("p j t -> p (j t)")
                     )
                     h_codes.append(codes)
                     h_scs.append(h_sc)

@@ -51,11 +51,13 @@ def tile_list_rvq_gelu_gelu_kernel(
         sc_raw = keep.tile([16, LISTS, R // 4], I32, name="sc_raw", align_bytes=64)
         for g in range(LISTS):
             nc.sync.dma_start(sc_raw[:, g, :], w_scales[g][0].bitcast(I32))
-        w_raw = []
-        for g in range(LISTS):
-            raw = keep.tile([P, R // 2], I32, name=f"w_raw{g}", tag=f"stage{g}", align_bytes=64)
+
+        def load_words(g):
+            raw = keep.tile([P, R // 2], I32, name=f"w_raw{g}", tag=f"stage{min(g, 1)}", align_bytes=64)
             nc.sync.dma_start(raw[:], w_words[g][0].bitcast(I32))
-            w_raw.append(raw)
+            return raw
+
+        w_raw = [load_words(0), load_words(1)]
         nc.sync.dma_start(table[:], tab_words[0].rearrange("p t i -> p (t i)").bitcast(I32))
         nc.vector.tensor_copy(
             w_sc[0:16, :].rearrange("p (g s q x) -> p g s q x", g=LISTS, s=SLOTS, x=2),
@@ -75,7 +77,7 @@ def tile_list_rvq_gelu_gelu_kernel(
             return offsets[:, first : first + CHUNK // 16]
 
         def gather_scales(c):
-            picked = keep.tile([P, LISTS * CHUNK], U8, name=f"picked_sc{c}", tag=("picked_sc", "stage0")[c], align_bytes=64)
+            picked = keep.tile([P, LISTS * CHUNK], U8, name=f"picked_sc{c}", tag=("picked_sc", "stage1")[c], align_bytes=64)
             for g in range(LISTS):
                 nc.vector.tensor_copy(
                     picked[:, g * CHUNK : (g + 1) * CHUNK], table_sc[:].bitcast(U8).indirect(list_slice(c, g))
@@ -98,7 +100,9 @@ def tile_list_rvq_gelu_gelu_kernel(
             return ordered
 
         gather_scales(0)
-        w_ord = [order_words(g) for g in range(LISTS)]
+        w_ord = [order_words(0), order_words(1)]
+        w_raw.append(load_words(2))
+        w_ord.append(order_words(2))
         picked_words = {}
         picked0 = keep.tile([P, LISTS, CHUNK], U32, name="picked0", align_bytes=64)
         for g in range(LISTS):
@@ -114,7 +118,7 @@ def tile_list_rvq_gelu_gelu_kernel(
         cols = keep.tile([P, 16], F32, name="cols")
         nc.scalar.copy(cols[:], turned[:, 0:16])
 
-        wd_raw = keep.tile([P, SLOTS, N], F32, name="wd_raw", tag="stage2", align_bytes=64)
+        wd_raw = keep.tile([P, SLOTS, N], F32, name="wd_raw", tag="picked_sc", align_bytes=64)
         wd_rows = wd.rearrange("(q s i) n -> i q s n", s=SLOTS, i=8)
         for i in range(8):
             nc.sync.dma_start(wd_raw[i:P:8, :, :], wd_rows[i])
@@ -206,13 +210,16 @@ def tile_list_rvq_gelu_gelu_kernel(
                     )
                     h_codes.append(codes)
                     h_scs.append(h_sc)
-                ybank = psum.tile([P, N // P, PIECE], F32, name=f"y{u}", tag=f"bank{6 + u % 2}")
-                result = keep.tile([P, N // P, PIECE], F32, name=f"result{u}")
+                ybanks = []
                 for m in range(N // P):
-                    for a in range(PASSES):
+                    ybank = psum.tile([P, PIECE], F32, name=f"y{u}_{m}", tag=f"bank{6 - 2 * (u % 2) + m}")
+                    ybanks.append(ybank)
+                result = keep.tile([P, N // P, PIECE], F32, name=f"result{u}")
+                for a in range(PASSES):
+                    for m in range(N // P):
                         first = a * N + m * P
                         nc.tensor.matmul_mx(
-                            out=ybank[:, m, :],
+                            out=ybanks[m][:],
                             lhsT=wd_codes[:, first : first + P].bitcast(FP8X4),
                             lhsT_scale=wd_sc[:, first : first + P],
                             rhs=h_codes[a][:].bitcast(FP8X4),
@@ -222,7 +229,7 @@ def tile_list_rvq_gelu_gelu_kernel(
                         )
                 for m in range(N // P):
                     nc.scalar.activation(
-                        result[:, m, :], ybank[:, m, :], GELU, bias=cols[:, SLOTS + m : SLOTS + m + 1]
+                        result[:, m, :], ybanks[m][:], GELU, bias=cols[:, SLOTS + m : SLOTS + m + 1]
                     )
                 j0 = c * CHUNK + h * PIECE
                 nc.sync.dma_start(out[:, j0 : j0 + PIECE].rearrange("(m p) j -> p m j", p=P), result[:])

@@ -16,16 +16,23 @@ U8 = mybir.dt.uint8
 FP8X4 = mybir.dt.float8_e4m3fn_x4
 FP4X4 = mybir.dt.float4_e2m1fn_x4
 GELU = mybir.ActivationFunctionType.Gelu_apprx_tanh
-COPY = mybir.ActivationFunctionType.Copy
 MULT = mybir.AluOpType.mult
 ADD = mybir.AluOpType.add
 
 P = 128
 PACK = 4
+RUN = 8
+QUADS = 4
+SCALE_ROWS = 16
+GROUP = 16
 PASSES = R // (P * PACK)
 SLOTS = PASSES * PACK
+BANKS = 7
 CHUNK = 512
 PIECE = 256
+GPSIMD_ZEROED = 5 * T // 32
+AHEAD = (2, 4)
+COLS = 16
 
 
 def tile_list_rvq_gelu_gelu_kernel(
@@ -40,15 +47,15 @@ def tile_list_rvq_gelu_gelu_kernel(
         keep = ctx.enter_context(tc.tile_pool(name="keep", bufs=1))
         psum = ctx.enter_context(tc.psum_pool(name="psum", bufs=1))
 
-        offsets = keep.tile([P, LISTS * J // 16], U16, name="offsets")
+        offsets = keep.tile([P, LISTS * J // GROUP], U16, name="offsets")
         table = keep.tile([P, T], I32, name="table", align_bytes=64)
         table_sc = keep.tile([P, T // 4], I32, name="table_sc", tag="table_sc", align_bytes=64)
-        nc.gpsimd.memset(table_sc[:, 0 : 5 * T // 32], 0)
-        nc.vector.memset(table_sc[:, 5 * T // 32 : T // 4], 0)
+        nc.gpsimd.memset(table_sc[:, 0:GPSIMD_ZEROED], 0)
+        nc.vector.memset(table_sc[:, GPSIMD_ZEROED : T // 4], 0)
         nc.sync.dma_start(offsets[:], offs)
-        nc.sync.dma_start(table_sc[0:P:8, :], tab_scales[0].bitcast(I32))
+        nc.sync.dma_start(table_sc[0:P:RUN, :], tab_scales[0].bitcast(I32))
         w_sc = keep.tile([P, LISTS * R // 4], I32, name="w_sc", align_bytes=64)
-        sc_raw = keep.tile([16, LISTS, R // 4], I32, name="sc_raw", align_bytes=64)
+        sc_raw = keep.tile([SCALE_ROWS, LISTS, R // 4], I32, name="sc_raw", align_bytes=64)
         for g in range(LISTS):
             nc.sync.dma_start(sc_raw[:, g, :], w_scales[g][0].bitcast(I32))
 
@@ -59,11 +66,12 @@ def tile_list_rvq_gelu_gelu_kernel(
 
         w_raw = [load_words(0), load_words(1)]
         nc.sync.dma_start(table[:], tab_words[0].rearrange("p t i -> p (t i)").bitcast(I32))
+
         nc.vector.tensor_copy(
-            w_sc[0:16, :].rearrange("p (g s q x) -> p g s q x", g=LISTS, s=SLOTS, x=2),
+            w_sc[0:SCALE_ROWS, :].rearrange("p (g s q x) -> p g s q x", g=LISTS, s=SLOTS, x=2),
             sc_raw[:].rearrange("p g (q s x) -> p g s q x", s=SLOTS, x=2),
         )
-        for quad in range(1, 4):
+        for quad in range(1, QUADS):
             nc.sync.dma_start(w_sc[32 * quad : 32 * quad + 4, :], w_sc[4 * quad : 4 * quad + 4, :])
         ident = keep.tile([P, P], F32, name="ident")
         make_identity(nc, ident[:])
@@ -73,18 +81,19 @@ def tile_list_rvq_gelu_gelu_kernel(
             planes.append(plane)
 
         def list_slice(c, g):
-            first = (g * J + c * CHUNK) // 16
-            return offsets[:, first : first + CHUNK // 16]
+            column = (g * J + c * CHUNK) // GROUP
+            return offsets[:, column : column + CHUNK // GROUP]
 
-        def gather_scales(c):
-            picked = keep.tile([P, LISTS * CHUNK], U8, name=f"picked_sc{c}", tag=("picked_sc", "stage1")[c], align_bytes=64)
+        def gather_scales(c, tag):
+            picked_sc = keep.tile([P, LISTS * CHUNK], U8, name=f"picked_sc{c}", tag=tag, align_bytes=64)
             for g in range(LISTS):
                 nc.vector.tensor_copy(
-                    picked[:, g * CHUNK : (g + 1) * CHUNK], table_sc[:].bitcast(U8).indirect(list_slice(c, g))
+                    picked_sc[:, g * CHUNK : (g + 1) * CHUNK], table_sc[:].bitcast(U8).indirect(list_slice(c, g))
                 )
-            for quad in range(4):
+            for quad in range(QUADS):
                 nc.sync.dma_start(
-                    planes[c][32 * quad : 32 * quad + 4, :], picked[:].bitcast(I32)[32 * quad : 32 * quad + 32 : 8, :]
+                    planes[c][32 * quad : 32 * quad + 4, :],
+                    picked_sc[:].bitcast(I32)[32 * quad : 32 * quad + 32 : RUN, :],
                 )
 
         def gather_words(c, g, picked):
@@ -99,7 +108,7 @@ def tile_list_rvq_gelu_gelu_kernel(
             )
             return ordered
 
-        gather_scales(0)
+        gather_scales(0, "picked_sc")
         w_ord = [order_words(0), order_words(1)]
         w_raw.append(load_words(2))
         w_ord.append(order_words(2))
@@ -107,28 +116,50 @@ def tile_list_rvq_gelu_gelu_kernel(
         picked0 = keep.tile([P, LISTS, CHUNK], U32, name="picked0", align_bytes=64)
         for g in range(LISTS):
             picked_words[0, g] = gather_words(0, g, picked0)
+
         rows = keep.tile([P, P], F32, name="rows", tag="stage0", align_bytes=64)
         nc.gpsimd.memset(rows[:], 0.0)
         nc.sync.dma_start(
-            rows[0:SLOTS, :].rearrange("s (q i) -> s q i", i=8), sm.rearrange("(q s i) -> s q i", s=SLOTS, i=8)
+            rows[0:SLOTS, :].rearrange("s (q i) -> s q i", i=RUN), sm.rearrange("(q s i) -> s q i", s=SLOTS, i=RUN)
         )
-        nc.sync.dma_start(rows[SLOTS : SLOTS + N // P, :], b.rearrange("(c p) -> c p", p=P))
-        turned = psum.tile([P, P], F32, name="turned", tag="bank7")
-        nc.tensor.transpose(turned[:], rows[:], ident[:])
-        cols = keep.tile([P, 16], F32, name="cols")
-        nc.scalar.copy(cols[:], turned[:, 0:16])
+        nc.sync.dma_start(rows[SLOTS : SLOTS + N // P, :], b.rearrange("(m p) -> m p", p=P))
+        turned = psum.tile([P, CHUNK], F32, name="turned", tag="vectors")
+        nc.tensor.transpose(turned[:, 0:P], rows[:], ident[:])
+        cols = keep.tile([P, COLS], F32, name="cols")
+        nc.scalar.copy(cols[:], turned[:, 0:COLS])
 
         wd_raw = keep.tile([P, SLOTS, N], F32, name="wd_raw", tag="picked_sc", align_bytes=64)
-        wd_rows = wd.rearrange("(q s i) n -> i q s n", s=SLOTS, i=8)
-        for i in range(8):
-            nc.sync.dma_start(wd_raw[i:P:8, :, :], wd_rows[i])
+        wd_rows = wd.rearrange("(q s i) n -> i q s n", s=SLOTS, i=RUN)
+        for i in range(RUN):
+            nc.sync.dma_start(wd_raw[i:P:RUN, :, :], wd_rows[i])
 
-        gather_scales(1)
+        gather_scales(1, "stage1")
         picked1 = keep.tile([P, LISTS, CHUNK], U32, name="picked1", tag="table_sc", align_bytes=64)
         for g in range(LISTS):
             picked_words[1, g] = gather_words(1, g, picked1)
 
+        def bank_of(c, s):
+            return f"bank{(c * SLOTS + s) % BANKS}"
+
         all_acts = []
+        woven_h = {}
+
+        def scale_and_weave(c, a, j_first, width):
+            scaled = keep.tile([P, PACK, width], BF16, name=f"scaled{c}", align_bytes=64)
+            woven = keep.tile([P, width, PACK], BF16, name=f"woven{c}", align_bytes=64)
+            for t in range(PACK):
+                s = a * PACK + t
+                nc.gpsimd.tensor_scalar(
+                    scaled[:, t, :], all_acts[c][a][:, t, j_first : j_first + width], cols[:, s : s + 1], 0.0, MULT, ADD
+                )
+            for j_piece in range(0, width, PIECE):
+                js = slice(j_piece, j_piece + PIECE)
+                nc.scalar.copy(
+                    woven[:, js, :].rearrange("p (z e) t -> p z t e", e=4),
+                    scaled[:, :, js].rearrange("p t (z e) -> p z t e", e=4),
+                )
+                woven_h[(c * CHUNK + j_first + j_piece) // PIECE, a] = woven[:, js, :]
+
         for c in range(chunks):
             acts = []
             for a in range(PASSES):
@@ -136,14 +167,12 @@ def tile_list_rvq_gelu_gelu_kernel(
                 act = keep.tile([P, PACK, CHUNK], F32, name=f"act{c}_{a}", tag=tag, align_bytes=64)
                 acts.append(act)
             all_acts.append(acts)
-            accs = []
-            for s in range(SLOTS):
-                acc = psum.tile([P, CHUNK], F32, name=f"acc{c}_{s}", tag=f"bank{s}")
-                accs.append(acc)
-            ahead = (2, 4)[c]
-            steps = [(s, g) for g in range(LISTS) for s in range(ahead)]
-            steps.extend([(s, g) for s in range(ahead, SLOTS) for g in range(LISTS)])
+            accs = {}
+            steps = [(s, g) for g in range(LISTS) for s in range(AHEAD[c])]
+            steps.extend([(s, g) for s in range(AHEAD[c], SLOTS) for g in range(LISTS)])
             for s, g in steps:
+                if g == 0:
+                    accs[s] = psum.tile([P, CHUNK], F32, name=f"acc{c}_{s}", tag=bank_of(c, s))
                 nc.tensor.matmul_mx(
                     out=accs[s][:],
                     lhsT=w_ord[g][:].bitcast(U8)[:, 2 * P * s : 2 * P * (s + 1)].bitcast(FP4X4),
@@ -156,16 +185,7 @@ def tile_list_rvq_gelu_gelu_kernel(
                 if g == LISTS - 1:
                     nc.scalar.activation(acts[s // PACK][:, s % PACK, :], accs[s][:], GELU)
             if c == 0:
-                scaled = keep.tile([P, PACK, CHUNK], BF16, name="scaled", align_bytes=64)
-                woven = keep.tile([P, CHUNK, PACK], BF16, name="woven", align_bytes=64)
-                for t in range(PACK):
-                    nc.gpsimd.tensor_scalar(scaled[:, t, :], acts[0][:, t, :], cols[:, t : t + 1], 0.0, MULT, ADD)
-                for h in range(CHUNK // PIECE):
-                    js = slice(h * PIECE, (h + 1) * PIECE)
-                    nc.scalar.copy(
-                        woven[:, js, :].rearrange("p (c e) t -> p c t e", e=4),
-                        scaled[:, :, js].rearrange("p t (c e) -> p c t e", e=4),
-                    )
+                scale_and_weave(0, 0, 0, CHUNK)
 
         wd_bf = keep.tile([P, PASSES, N, PACK], BF16, name="wd_bf", tag="wd_bf", align_bytes=64)
         for a in range(PASSES):
@@ -178,26 +198,28 @@ def tile_list_rvq_gelu_gelu_kernel(
             out=wd_codes[:].bitcast(FP8X4), scales=wd_sc[:], in_=wd_bf[:].rearrange("p a n t -> p (a n t)")
         )
 
+        scale_and_weave(chunks - 1, PASSES - 1, CHUNK - PIECE, PIECE)
+
         for c in range(chunks):
             acts = all_acts[c]
             h_all = keep.tile(
                 [P, PASSES, CHUNK, PACK], BF16, name=f"h_all{c}", tag=("h_all", "wd_bf")[c], align_bytes=64
             )
-            for h in range(CHUNK // PIECE):
-                js = slice(h * PIECE, (h + 1) * PIECE)
-                u = c * (CHUNK // PIECE) + h
+            for half in range(CHUNK // PIECE):
+                js = slice(half * PIECE, (half + 1) * PIECE)
+                u = c * (CHUNK // PIECE) + half
                 h_codes = []
                 h_scs = []
                 h_bfs = []
                 for a in range(PASSES):
-                    if (c, a) == (0, 0):
-                        h_bfs.append(woven[:, js, :])
+                    if (u, a) in woven_h:
+                        h_bfs.append(woven_h[u, a])
                         continue
                     h_bf = h_all[:, a, js, :]
-                    factor = cols[:, a * PACK : (a + 1) * PACK].unsqueeze(1).unsqueeze(3)
+                    factor = turned[:, a * PACK : (a + 1) * PACK].unsqueeze(1).unsqueeze(3)
                     nc.vector.tensor_tensor(
-                        h_bf.rearrange("p (c e) t -> p c t e", e=2),
-                        acts[a][:, :, js].rearrange("p t (c e) -> p c t e", e=2),
+                        h_bf.rearrange("p (z e) t -> p z t e", e=2),
+                        acts[a][:, :, js].rearrange("p t (z e) -> p z t e", e=2),
                         factor.to_broadcast([P, PIECE // 2, PACK, 2]),
                         MULT,
                     )
@@ -212,7 +234,8 @@ def tile_list_rvq_gelu_gelu_kernel(
                     h_scs.append(h_sc)
                 ybanks = []
                 for m in range(N // P):
-                    ybank = psum.tile([P, PIECE], F32, name=f"y{u}_{m}", tag=f"bank{6 - 2 * (u % 2) + m}")
+                    follows = SLOTS - (N // P) * (1 + u % 2) + m
+                    ybank = psum.tile([P, PIECE], F32, name=f"y{u}_{m}", tag=bank_of(chunks - 1, follows))
                     ybanks.append(ybank)
                 result = keep.tile([P, N // P, PIECE], F32, name=f"result{u}")
                 for a in range(PASSES):
@@ -231,5 +254,5 @@ def tile_list_rvq_gelu_gelu_kernel(
                     nc.scalar.activation(
                         result[:, m, :], ybanks[m][:], GELU, bias=cols[:, SLOTS + m : SLOTS + m + 1]
                     )
-                j0 = c * CHUNK + h * PIECE
+                j0 = u * PIECE
                 nc.sync.dma_start(out[:, j0 : j0 + PIECE].rearrange("(m p) j -> p m j", p=P), result[:])

@@ -32,7 +32,7 @@ CHUNK = 512
 PIECE = 256
 GPSIMD_ZEROED = 5 * T // 32
 AHEAD = (2, 4)
-COLS = 16
+COLS = 8
 
 
 def tile_list_rvq_gelu_gelu_kernel(
@@ -45,6 +45,7 @@ def tile_list_rvq_gelu_gelu_kernel(
 
     with ExitStack() as ctx:
         keep = ctx.enter_context(tc.tile_pool(name="keep", bufs=1))
+        stage = ctx.enter_context(tc.tile_pool(name="stage", bufs=1))
         psum = ctx.enter_context(tc.psum_pool(name="psum", bufs=1))
 
         offsets = keep.tile([P, LISTS * J // GROUP], U16, name="offsets")
@@ -53,19 +54,25 @@ def tile_list_rvq_gelu_gelu_kernel(
         nc.gpsimd.memset(table_sc[:, 0:GPSIMD_ZEROED], 0)
         nc.vector.memset(table_sc[:, GPSIMD_ZEROED : T // 4], 0)
         nc.sync.dma_start(offsets[:], offs)
-        nc.sync.dma_start(table_sc[0:P:RUN, :], tab_scales[0].bitcast(I32))
         w_sc = keep.tile([P, LISTS * R // 4], I32, name="w_sc", align_bytes=64)
         sc_raw = keep.tile([SCALE_ROWS, LISTS, R // 4], I32, name="sc_raw", align_bytes=64)
         for g in range(LISTS):
             nc.sync.dma_start(sc_raw[:, g, :], w_scales[g][0].bitcast(I32))
 
         def load_words(g):
-            raw = keep.tile([P, R // 2], I32, name=f"w_raw{g}", tag=f"stage{min(g, 1)}", align_bytes=64)
+            raw = stage.tile([P, R // 2], I32, name=f"w_raw{g}", offset=(3 * R, 0, 2 * R)[g], align_bytes=64)
             nc.sync.dma_start(raw[:], w_words[g][0].bitcast(I32))
             return raw
 
-        w_raw = [load_words(0), load_words(1)]
+        rows = keep.tile([P, P], F32, name="rows", align_bytes=64)
+        nc.gpsimd.memset(rows[:], 0.0)
+        nc.sync.dma_start(
+            rows[0:SLOTS, :].rearrange("s (q i) -> s q i", i=RUN), sm.rearrange("(q s i) -> s q i", s=SLOTS, i=RUN)
+        )
+        nc.sync.dma_start(table_sc[0:P:RUN, :], tab_scales[0].bitcast(I32))
+        w_raw = [load_words(0)]
         nc.sync.dma_start(table[:], tab_words[0].rearrange("p t i -> p (t i)").bitcast(I32))
+        w_raw.append(load_words(1))
 
         nc.vector.tensor_copy(
             w_sc[0:SCALE_ROWS, :].rearrange("p (g s q x) -> p g s q x", g=LISTS, s=SLOTS, x=2),
@@ -73,8 +80,16 @@ def tile_list_rvq_gelu_gelu_kernel(
         )
         for quad in range(1, QUADS):
             nc.sync.dma_start(w_sc[32 * quad : 32 * quad + 4, :], w_sc[4 * quad : 4 * quad + 4, :])
+        bias = keep.tile([P, N // P], F32, name="bias")
+        with nc.allow_non_contiguous_dma(reason="one bias value a partition"):
+            nc.gpsimd.dma_start(bias[:], b.rearrange("(m p) -> p m", p=P))
         ident = keep.tile([P, P], F32, name="ident")
         make_identity(nc, ident[:])
+        turned = psum.tile([P, CHUNK], F32, name="turned", tag="vectors")
+        nc.tensor.transpose(turned[:, 0:P], rows[:], ident[:])
+        cols = keep.tile([P, COLS], F32, name="cols")
+        nc.vector.tensor_copy(cols[:], turned[:, 0:COLS])
+
         planes = []
         for c in range(chunks):
             plane = keep.tile([P, LISTS * CHUNK // 4], I32, name=f"plane{c}", align_bytes=64)
@@ -84,59 +99,48 @@ def tile_list_rvq_gelu_gelu_kernel(
             column = (g * J + c * CHUNK) // GROUP
             return offsets[:, column : column + CHUNK // GROUP]
 
-        def gather_scales(c, tag):
-            picked_sc = keep.tile([P, LISTS * CHUNK], U8, name=f"picked_sc{c}", tag=tag, align_bytes=64)
+        def gather_scales(c, picked_sc):
             for g in range(LISTS):
                 nc.vector.tensor_copy(
                     picked_sc[:, g * CHUNK : (g + 1) * CHUNK], table_sc[:].bitcast(U8).indirect(list_slice(c, g))
                 )
-            for quad in range(QUADS):
-                nc.sync.dma_start(
-                    planes[c][32 * quad : 32 * quad + 4, :],
-                    picked_sc[:].bitcast(I32)[32 * quad : 32 * quad + 32 : RUN, :],
-                )
+            if c == 0:
+                nc.vector.tensor_copy(planes[c][:], picked_sc[:].bitcast(I32))
+            for x in range(1 - c, QUADS):
+                nc.sync.dma_start(planes[c][x:P:32, :], picked_sc[:].bitcast(I32)[RUN * x : P : 32, :])
 
         def gather_words(c, g, picked):
-            nc.vector.tensor_copy(picked[:, g, :], table[:].bitcast(U32).indirect(list_slice(c, g)))
-            return picked[:, g, :]
+            nc.vector.tensor_copy(picked, table[:].bitcast(U32).indirect(list_slice(c, g)))
+            return picked
 
         def order_words(g):
             ordered = keep.tile([P, R // 2], I32, name=f"w_ord{g}", align_bytes=64)
-            nc.vector.tensor_copy(
+            (nc.vector if g == 0 else nc.gpsimd).tensor_copy(
                 ordered[:].rearrange("p (s q x) -> p s q x", s=SLOTS, x=4),
                 w_raw[g][:].rearrange("p (q s x) -> p s q x", s=SLOTS, x=4),
             )
             return ordered
 
-        gather_scales(0, "picked_sc")
-        w_ord = [order_words(0), order_words(1)]
+        picked_sc0 = stage.tile([P, LISTS * CHUNK], U8, name="picked_sc0", offset=12 * R, align_bytes=64)
+        gather_scales(0, picked_sc0)
+        w_ord = [order_words(0)]
         w_raw.append(load_words(2))
-        w_ord.append(order_words(2))
         picked_words = {}
         picked0 = keep.tile([P, LISTS, CHUNK], U32, name="picked0", align_bytes=64)
         for g in range(LISTS):
-            picked_words[0, g] = gather_words(0, g, picked0)
+            picked_words[0, g] = gather_words(0, g, picked0[:, g, :])
+        w_ord.extend([order_words(1), order_words(2)])
 
-        rows = keep.tile([P, P], F32, name="rows", tag="stage0", align_bytes=64)
-        nc.gpsimd.memset(rows[:], 0.0)
-        nc.sync.dma_start(
-            rows[0:SLOTS, :].rearrange("s (q i) -> s q i", i=RUN), sm.rearrange("(q s i) -> s q i", s=SLOTS, i=RUN)
-        )
-        nc.sync.dma_start(rows[SLOTS : SLOTS + N // P, :], b.rearrange("(m p) -> m p", p=P))
-        turned = psum.tile([P, CHUNK], F32, name="turned", tag="vectors")
-        nc.tensor.transpose(turned[:, 0:P], rows[:], ident[:])
-        cols = keep.tile([P, COLS], F32, name="cols")
-        nc.scalar.copy(cols[:], turned[:, 0:COLS])
-
-        wd_raw = keep.tile([P, SLOTS, N], F32, name="wd_raw", tag="picked_sc", align_bytes=64)
+        wd_raw = stage.tile([P, SLOTS, N], F32, name="wd_raw", offset=4 * R, align_bytes=64)
         wd_rows = wd.rearrange("(q s i) n -> i q s n", s=SLOTS, i=RUN)
-        for i in range(RUN):
+        for i in [x + half for x in range(RUN // 2) for half in (0, RUN // 2)]:
             nc.sync.dma_start(wd_raw[i:P:RUN, :, :], wd_rows[i])
 
-        gather_scales(1, "stage1")
+        picked_sc1 = stage.tile([P, LISTS * CHUNK], U8, name="picked_sc1", offset=2 * R, align_bytes=64)
+        gather_scales(1, picked_sc1)
         picked1 = keep.tile([P, LISTS, CHUNK], U32, name="picked1", tag="table_sc", align_bytes=64)
         for g in range(LISTS):
-            picked_words[1, g] = gather_words(1, g, picked1)
+            picked_words[1, g] = gather_words(1, g, picked1[:, g, :])
 
         def bank_of(c, s):
             return f"bank{(c * SLOTS + s) % BANKS}"
@@ -252,7 +256,7 @@ def tile_list_rvq_gelu_gelu_kernel(
                         )
                 for m in range(N // P):
                     nc.scalar.activation(
-                        result[:, m, :], ybanks[m][:], GELU, bias=cols[:, SLOTS + m : SLOTS + m + 1]
+                        result[:, m, :], ybanks[m][:], GELU, bias=bias[:, m : m + 1]
                     )
                 j0 = u * PIECE
                 nc.sync.dma_start(out[:, j0 : j0 + PIECE].rearrange("(m p) j -> p m j", p=P), result[:])

@@ -60,7 +60,7 @@ def tile_list_rvq_gelu_gelu_kernel(
             nc.sync.dma_start(sc_raw[:, g, :], w_scales[g][0].bitcast(I32))
 
         def load_words(g):
-            raw = stage.tile([P, R // 2], I32, name=f"w_raw{g}", offset=(3 * R, 0, 2 * R)[g], align_bytes=64)
+            raw = stage.tile([P, R // 2], I32, name=f"w_raw{g}", offset=(3 * R + CHUNK, 0, 2 * R)[g], align_bytes=64)
             nc.sync.dma_start(raw[:], w_words[g][0].bitcast(I32))
             return raw
 
@@ -99,15 +99,18 @@ def tile_list_rvq_gelu_gelu_kernel(
             column = (g * J + c * CHUNK) // GROUP
             return offsets[:, column : column + CHUNK // GROUP]
 
-        def gather_scales(c, picked_sc):
-            for g in range(LISTS):
+        def gather_scales(c, picked_sc, lists):
+            for n, g in enumerate(lists):
                 nc.vector.tensor_copy(
-                    picked_sc[:, g * CHUNK : (g + 1) * CHUNK], table_sc[:].bitcast(U8).indirect(list_slice(c, g))
+                    picked_sc[:, n * CHUNK : (n + 1) * CHUNK], table_sc[:].bitcast(U8).indirect(list_slice(c, g))
                 )
+
+        def move_scales(c, picked_sc, lists):
+            columns = slice(lists[0] * CHUNK // 4, (lists[-1] + 1) * CHUNK // 4)
             if c == 0:
                 nc.vector.tensor_copy(planes[c][:], picked_sc[:].bitcast(I32))
             for x in range(1 - c, QUADS):
-                nc.sync.dma_start(planes[c][x:P:32, :], picked_sc[:].bitcast(I32)[RUN * x : P : 32, :])
+                nc.sync.dma_start(planes[c][x:P:32, columns], picked_sc[:].bitcast(I32)[RUN * x : P : 32, :])
 
         def gather_words(c, g, picked):
             nc.vector.tensor_copy(picked, table[:].bitcast(U32).indirect(list_slice(c, g)))
@@ -121,23 +124,28 @@ def tile_list_rvq_gelu_gelu_kernel(
             )
             return ordered
 
-        picked_sc0 = stage.tile([P, LISTS * CHUNK], U8, name="picked_sc0", offset=12 * R, align_bytes=64)
-        gather_scales(0, picked_sc0)
+        picked_sc0 = stage.tile([P, LISTS * CHUNK], U8, name="picked_sc0", offset=13 * R, align_bytes=64)
+        gather_scales(0, picked_sc0, (0, 1, 2))
+        move_scales(0, picked_sc0, (0, 1, 2))
         w_ord = [order_words(0)]
+        picked_sc10 = stage.tile([P, CHUNK], U8, name="picked_sc10", offset=4 * R, align_bytes=64)
         w_raw.append(load_words(2))
+        gather_scales(1, picked_sc10, (0,))
         picked_words = {}
         picked0 = keep.tile([P, LISTS, CHUNK], U32, name="picked0", align_bytes=64)
         for g in range(LISTS):
             picked_words[0, g] = gather_words(0, g, picked0[:, g, :])
         w_ord.extend([order_words(1), order_words(2)])
 
-        wd_raw = stage.tile([P, SLOTS, N], F32, name="wd_raw", offset=4 * R, align_bytes=64)
+        wd_raw = stage.tile([P, SLOTS, N], F32, name="wd_raw", offset=4 * R + CHUNK, align_bytes=64)
         wd_rows = wd.rearrange("(q s i) n -> i q s n", s=SLOTS, i=RUN)
         for i in [x + half for x in range(RUN // 2) for half in (0, RUN // 2)]:
             nc.sync.dma_start(wd_raw[i:P:RUN, :, :], wd_rows[i])
 
-        picked_sc1 = stage.tile([P, LISTS * CHUNK], U8, name="picked_sc1", offset=2 * R, align_bytes=64)
-        gather_scales(1, picked_sc1)
+        picked_sc1 = stage.tile([P, 2 * CHUNK], U8, name="picked_sc1", offset=2 * R, align_bytes=64)
+        move_scales(1, picked_sc10, (0,))
+        gather_scales(1, picked_sc1, (1, 2))
+        move_scales(1, picked_sc1, (1, 2))
         picked1 = keep.tile([P, LISTS, CHUNK], U32, name="picked1", tag="table_sc", align_bytes=64)
         for g in range(LISTS):
             picked_words[1, g] = gather_words(1, g, picked1[:, g, :])
@@ -146,30 +154,46 @@ def tile_list_rvq_gelu_gelu_kernel(
             return f"bank{(c * SLOTS + s) % BANKS}"
 
         all_acts = []
-        woven_h = {}
 
-        def scale_and_weave(c, a, j_first, width):
-            scaled = keep.tile([P, PACK, width], BF16, name=f"scaled{c}", align_bytes=64)
-            woven = keep.tile([P, width, PACK], BF16, name=f"woven{c}", align_bytes=64)
+        def scale_in_pairs(c, a, j_first, width, weaver):
+            scaled = keep.tile([P, PACK // 2, width, 2], BF16, name=f"scaled{c}_{a}", tag=f"scaled{c}_{a}", align_bytes=64)
+            woven = keep.tile([P, width, PACK], BF16, name=f"woven{c}_{a}", tag=f"woven{c}_{a}", align_bytes=64)
             for t in range(PACK):
                 s = a * PACK + t
                 nc.gpsimd.tensor_scalar(
-                    scaled[:, t, :], all_acts[c][a][:, t, j_first : j_first + width], cols[:, s : s + 1], 0.0, MULT, ADD
+                    scaled[:, t // 2, :, t % 2],
+                    all_acts[c][a][:, t, j_first : j_first + width],
+                    cols[:, s : s + 1],
+                    0.0,
+                    MULT,
+                    ADD,
                 )
-            for j_piece in range(0, width, PIECE):
-                js = slice(j_piece, j_piece + PIECE)
-                nc.scalar.copy(
-                    woven[:, js, :].rearrange("p (z e) t -> p z t e", e=4),
-                    scaled[:, :, js].rearrange("p t (z e) -> p z t e", e=4),
-                )
-                woven_h[(c * CHUNK + j_first + j_piece) // PIECE, a] = woven[:, js, :]
+            weaver(woven[:].bitcast(U32), scaled[:].bitcast(U32).rearrange("p u j x -> p j (u x)"))
+            return woven
 
+        def scale_on_vector(c, a, j_first, width):
+            woven = keep.tile([P, width, PACK], BF16, name=f"h{c}_{a}_{j_first}", tag=("scaled0_1", "act1_0")[a], align_bytes=64)
+            factor = turned[:, a * PACK : (a + 1) * PACK].unsqueeze(1).unsqueeze(3)
+            nc.vector.tensor_tensor(
+                woven[:].rearrange("p (z e) t -> p z t e", e=2),
+                all_acts[c][a][:, :, j_first : j_first + width].rearrange("p t (z e) -> p z t e", e=2),
+                factor.to_broadcast([P, width // 2, PACK, 2]),
+                MULT,
+            )
+            return woven
+
+        def quantise(name, values, width, tag=None):
+            if name == "h0_0":
+                codes = stage.tile([P, width], U32, name="h0_0_codes", offset=6 * R, align_bytes=64)
+            else:
+                codes = keep.tile([P, width], U32, name=f"{name}_codes", tag=tag or f"{name}_codes", align_bytes=64)
+            plane = keep.tile([P, width], U8, name=f"{name}_sc", align_bytes=64)
+            nc.vector.quantize_mx(out=codes[:].bitcast(FP8X4), scales=plane[:], in_=values)
+            return codes, plane
+
+        woven0 = []
         for c in range(chunks):
-            acts = []
-            for a in range(PASSES):
-                tag = "wd_bf" if (c, a) == (0, 0) else f"act{c}_{a}"
-                act = keep.tile([P, PACK, CHUNK], F32, name=f"act{c}_{a}", tag=tag, align_bytes=64)
-                acts.append(act)
+            acts = [keep.tile([P, PACK, CHUNK], F32, name=f"act{c}_{a}", tag=f"act{c}_{a}", align_bytes=64) for a in range(PASSES)]
             all_acts.append(acts)
             accs = {}
             steps = [(s, g) for g in range(LISTS) for s in range(AHEAD[c])]
@@ -189,74 +213,42 @@ def tile_list_rvq_gelu_gelu_kernel(
                 if g == LISTS - 1:
                     nc.scalar.activation(acts[s // PACK][:, s % PACK, :], accs[s][:], GELU)
             if c == 0:
-                scale_and_weave(0, 0, 0, CHUNK)
-
-        wd_bf = keep.tile([P, PASSES, N, PACK], BF16, name="wd_bf", tag="wd_bf", align_bytes=64)
-        for a in range(PASSES):
-            nc.gpsimd.tensor_scalar(
-                wd_bf[:, a], wd_raw[:, a * PACK : (a + 1) * PACK, :].rearrange("p t n -> p n t"), 1.0, 0.0, MULT, ADD
-            )
-        wd_codes = keep.tile([P, PASSES * N], U32, name="wd_codes", align_bytes=64)
-        wd_sc = keep.tile([P, PASSES * N], U8, name="wd_sc", align_bytes=64)
-        nc.vector.quantize_mx(
-            out=wd_codes[:].bitcast(FP8X4), scales=wd_sc[:], in_=wd_bf[:].rearrange("p a n t -> p (a n t)")
-        )
-
-        scale_and_weave(chunks - 1, PASSES - 1, CHUNK - PIECE, PIECE)
-
-        for c in range(chunks):
-            acts = all_acts[c]
-            h_all = keep.tile(
-                [P, PASSES, CHUNK, PACK], BF16, name=f"h_all{c}", tag=("h_all", "wd_bf")[c], align_bytes=64
-            )
-            for half in range(CHUNK // PIECE):
-                js = slice(half * PIECE, (half + 1) * PIECE)
-                u = c * (CHUNK // PIECE) + half
-                h_codes = []
-                h_scs = []
-                h_bfs = []
+                woven0.append(scale_in_pairs(0, 0, 0, CHUNK, nc.scalar.copy))
+                wd_bf = keep.tile([P, PASSES, N, PACK], BF16, name="wd_bf", tag="woven0_1", align_bytes=64)
                 for a in range(PASSES):
-                    if (u, a) in woven_h:
-                        h_bfs.append(woven_h[u, a])
-                        continue
-                    h_bf = h_all[:, a, js, :]
-                    factor = turned[:, a * PACK : (a + 1) * PACK].unsqueeze(1).unsqueeze(3)
-                    nc.vector.tensor_tensor(
-                        h_bf.rearrange("p (z e) t -> p z t e", e=2),
-                        acts[a][:, :, js].rearrange("p t (z e) -> p z t e", e=2),
-                        factor.to_broadcast([P, PIECE // 2, PACK, 2]),
-                        MULT,
-                    )
-                    h_bfs.append(h_bf)
-                for a in range(PASSES):
-                    codes = keep.tile([P, PIECE], U32, name=f"h_codes{u}_{a}", align_bytes=64)
-                    h_sc = keep.tile([P, PIECE], U8, name=f"h_sc{u}_{a}", align_bytes=64)
-                    nc.vector.quantize_mx(
-                        out=codes[:].bitcast(FP8X4), scales=h_sc[:], in_=h_bfs[a].rearrange("p j t -> p (j t)")
-                    )
-                    h_codes.append(codes)
-                    h_scs.append(h_sc)
-                ybanks = []
+                    nc.vector.tensor_copy(wd_bf[:, a], wd_raw[:, a * PACK : (a + 1) * PACK, :].rearrange("p t n -> p n t"))
+                flat = "p j t -> p (j t)"
+                wd_codes, wd_sc = quantise("wd", wd_bf[:].rearrange("p a n t -> p (a n t)"), PASSES * N)
+                woven0.append(scale_in_pairs(0, 1, 0, CHUNK, nc.vector.tensor_copy))
+
+        h0 = [quantise(f"h0_{a}", woven0[a][:].rearrange(flat), CHUNK) for a in range(PASSES)]
+        woven10 = scale_on_vector(1, 0, 0, CHUNK)
+        h10 = quantise("h1_0", woven10[:].rearrange(flat), CHUNK)
+        last_woven = scale_in_pairs(1, 1, PIECE, PIECE, nc.scalar.copy)
+        h11 = [quantise("h1_1a", scale_on_vector(1, 1, 0, PIECE)[:].rearrange(flat), PIECE)]
+        h11.append(quantise("h1_1b", last_woven[:].rearrange(flat), PIECE, "act1_1"))
+
+        def second_layer(j0, width, operands, follows):
+            ybanks = [psum.tile([P, width], F32, name=f"y{j0}_{m}", tag=bank_of(1, follows[m])) for m in range(N // P)]
+            for a in range(PASSES):
                 for m in range(N // P):
-                    follows = SLOTS - (N // P) * (1 + u % 2) + m
-                    ybank = psum.tile([P, PIECE], F32, name=f"y{u}_{m}", tag=bank_of(chunks - 1, follows))
-                    ybanks.append(ybank)
-                result = keep.tile([P, N // P, PIECE], F32, name=f"result{u}")
-                for a in range(PASSES):
-                    for m in range(N // P):
-                        first = a * N + m * P
-                        nc.tensor.matmul_mx(
-                            out=ybanks[m][:],
-                            lhsT=wd_codes[:, first : first + P].bitcast(FP8X4),
-                            lhsT_scale=wd_sc[:, first : first + P],
-                            rhs=h_codes[a][:].bitcast(FP8X4),
-                            rhs_scale=h_scs[a][:],
-                            start=(a == 0),
-                            stop=(a == PASSES - 1),
-                        )
-                for m in range(N // P):
-                    nc.scalar.activation(
-                        result[:, m, :], ybanks[m][:], GELU, bias=bias[:, m : m + 1]
+                    first = a * N + m * P
+                    nc.tensor.matmul_mx(
+                        out=ybanks[m][:],
+                        lhsT=wd_codes[:, first : first + P].bitcast(FP8X4),
+                        lhsT_scale=wd_sc[:, first : first + P],
+                        rhs=operands[a][0].bitcast(FP8X4),
+                        rhs_scale=operands[a][1],
+                        start=(a == 0),
+                        stop=(a == PASSES - 1),
                     )
-                j0 = u * PIECE
-                nc.sync.dma_start(out[:, j0 : j0 + PIECE].rearrange("(m p) j -> p m j", p=P), result[:])
+            for m in range(N // P):
+                result = keep.tile([P, width], F32, name=f"result{j0}_{m}")
+                nc.scalar.activation(result[:], ybanks[m][:], GELU, bias=bias[:, m : m + 1])
+                nc.sync.dma_start(out[m * P : (m + 1) * P, j0 : j0 + width], result[:])
+
+        second_layer(0, CHUNK, [(codes[:], plane[:]) for codes, plane in h0], (5, 6))
+        for half in range(CHUNK // PIECE):
+            js = slice(half * PIECE, (half + 1) * PIECE)
+            operands = [(h10[0][:, js], h10[1][:, js]), (h11[half][0][:], h11[half][1][:])]
+            second_layer(CHUNK + half * PIECE, PIECE, operands, (1 + 2 * half, 2 + 2 * half))

@@ -49,51 +49,38 @@ def tile_list_rvq_gelu_gelu_kernel(
         psum = ctx.enter_context(tc.psum_pool(name="psum", bufs=1))
 
         offsets = keep.tile([P, LISTS * J // GROUP], U16, name="offsets")
-        table = keep.tile([P, T], I32, name="table", align_bytes=64)
+        table = stage.tile([P, T], I32, name="table", offset=20 * R, align_bytes=64)
         table_sc = keep.tile([P, T // 4], I32, name="table_sc", tag="table_sc", align_bytes=64)
-        nc.gpsimd.memset(table_sc[:, 0:GPSIMD_ZEROED], 0)
-        nc.vector.memset(table_sc[:, GPSIMD_ZEROED : T // 4], 0)
         nc.sync.dma_start(offsets[:], offs)
+        nc.sync.dma_start(table_sc[P - SCALE_ROWS : P, :], tab_scales[0].bitcast(I32))
+        rows = keep.tile([P, P], F32, name="rows", align_bytes=64)
+        nc.gpsimd.memset(rows[:], 0.0)
+        nc.gpsimd.dma_start(
+            rows[0:SLOTS, :].rearrange("s (q i) -> s q i", i=RUN), sm.rearrange("(q s i) -> s q i", s=SLOTS, i=RUN)
+        )
+        nc.vector.memset(table_sc[0 : P - SCALE_ROWS, :], 0)
         w_sc = keep.tile([P, LISTS * R // 4], I32, name="w_sc", align_bytes=64)
         sc_raw = keep.tile([SCALE_ROWS, LISTS, R // 4], I32, name="sc_raw", align_bytes=64)
         for g in range(LISTS):
             nc.sync.dma_start(sc_raw[:, g, :], w_scales[g][0].bitcast(I32))
 
         def load_words(g):
-            raw = stage.tile([P, R // 2], I32, name=f"w_raw{g}", offset=(3 * R + CHUNK, 0, 2 * R)[g], align_bytes=64)
+            raw = stage.tile([P, R // 2], I32, name=f"w_raw{g}", offset=(0, 4 * R - 64, 2 * R)[g], align_bytes=64)
             nc.sync.dma_start(raw[:], w_words[g][0].bitcast(I32))
             return raw
 
-        rows = keep.tile([P, P], F32, name="rows", align_bytes=64)
-        nc.gpsimd.memset(rows[:], 0.0)
-        nc.sync.dma_start(
-            rows[0:SLOTS, :].rearrange("s (q i) -> s q i", i=RUN), sm.rearrange("(q s i) -> s q i", s=SLOTS, i=RUN)
-        )
-        nc.sync.dma_start(table_sc[0:P:RUN, :], tab_scales[0].bitcast(I32))
-        w_raw = [load_words(0)]
+        w_raw = [load_words(0), load_words(1)]
         nc.sync.dma_start(table[:], tab_words[0].rearrange("p t i -> p (t i)").bitcast(I32))
-        w_raw.append(load_words(1))
 
-        nc.vector.tensor_copy(
-            w_sc[0:SCALE_ROWS, :].rearrange("p (g s q x) -> p g s q x", g=LISTS, s=SLOTS, x=2),
-            sc_raw[:].rearrange("p g (q s x) -> p g s q x", s=SLOTS, x=2),
-        )
-        for quad in range(1, QUADS):
-            nc.sync.dma_start(w_sc[32 * quad : 32 * quad + 4, :], w_sc[4 * quad : 4 * quad + 4, :])
-        bias = keep.tile([P, N // P], F32, name="bias")
-        with nc.allow_non_contiguous_dma(reason="one bias value a partition"):
-            nc.gpsimd.dma_start(bias[:], b.rearrange("(m p) -> p m", p=P))
         ident = keep.tile([P, P], F32, name="ident")
         make_identity(nc, ident[:])
         turned = psum.tile([P, CHUNK], F32, name="turned", tag="vectors")
         nc.tensor.transpose(turned[:, 0:P], rows[:], ident[:])
-        cols = keep.tile([P, COLS], F32, name="cols")
-        nc.vector.tensor_copy(cols[:], turned[:, 0:COLS])
 
-        planes = []
-        for c in range(chunks):
-            plane = keep.tile([P, LISTS * CHUNK // 4], I32, name=f"plane{c}", align_bytes=64)
-            planes.append(plane)
+        nc.gpsimd.tensor_copy(
+            w_sc[0:SCALE_ROWS, :].rearrange("p (g s q x) -> p g s q x", g=LISTS, s=SLOTS, x=2),
+            sc_raw[:].rearrange("p g (q s x) -> p g s q x", s=SLOTS, x=2),
+        )
 
         def list_slice(c, g):
             column = (g * J + c * CHUNK) // GROUP
@@ -107,10 +94,11 @@ def tile_list_rvq_gelu_gelu_kernel(
 
         def move_scales(c, picked_sc, lists):
             columns = slice(lists[0] * CHUNK // 4, (lists[-1] + 1) * CHUNK // 4)
-            if c == 0:
-                nc.vector.tensor_copy(planes[c][:], picked_sc[:].bitcast(I32))
-            for x in range(1 - c, QUADS):
-                nc.sync.dma_start(planes[c][x:P:32, columns], picked_sc[:].bitcast(I32)[RUN * x : P : 32, :])
+            for quad in range(QUADS):
+                first = P - SCALE_ROWS + 4 * quad
+                nc.sync.dma_start(
+                    planes[c][32 * quad : 32 * quad + 4, columns], picked_sc[:].bitcast(I32)[first : first + 4, :]
+                )
 
         def gather_words(c, g, picked):
             nc.vector.tensor_copy(picked, table[:].bitcast(U32).indirect(list_slice(c, g)))
@@ -118,34 +106,43 @@ def tile_list_rvq_gelu_gelu_kernel(
 
         def order_words(g):
             ordered = keep.tile([P, R // 2], I32, name=f"w_ord{g}", align_bytes=64)
-            (nc.vector if g == 0 else nc.gpsimd).tensor_copy(
+            nc.gpsimd.tensor_copy(
                 ordered[:].rearrange("p (s q x) -> p s q x", s=SLOTS, x=4),
                 w_raw[g][:].rearrange("p (q s x) -> p s q x", s=SLOTS, x=4),
             )
             return ordered
 
-        picked_sc0 = stage.tile([P, LISTS * CHUNK], U8, name="picked_sc0", offset=13 * R, align_bytes=64)
+        planes = [keep.tile([P, LISTS * CHUNK // 4], I32, name="plane0", align_bytes=64)]
+        picked_sc0 = keep.tile([P, LISTS * CHUNK], U8, name="picked_sc0", align_bytes=64)
         gather_scales(0, picked_sc0, (0, 1, 2))
         move_scales(0, picked_sc0, (0, 1, 2))
-        w_ord = [order_words(0)]
-        picked_sc10 = stage.tile([P, CHUNK], U8, name="picked_sc10", offset=4 * R, align_bytes=64)
+        for quad in range(1, QUADS):
+            nc.sync.dma_start(w_sc[32 * quad : 32 * quad + 4, :], w_sc[4 * quad : 4 * quad + 4, :])
+        w_ord = [order_words(0), order_words(1)]
         w_raw.append(load_words(2))
-        gather_scales(1, picked_sc10, (0,))
+        picked_sc1a = keep.tile([P, 2 * CHUNK], U8, name="picked_sc1a", align_bytes=64)
+        gather_scales(1, picked_sc1a, (0, 1))
         picked_words = {}
         picked0 = keep.tile([P, LISTS, CHUNK], U32, name="picked0", align_bytes=64)
         for g in range(LISTS):
             picked_words[0, g] = gather_words(0, g, picked0[:, g, :])
-        w_ord.extend([order_words(1), order_words(2)])
+        cols = keep.tile([P, COLS], F32, name="cols")
+        nc.vector.tensor_copy(cols[:], turned[:, 0:COLS])
+        w_ord.append(order_words(2))
+        bias = keep.tile([P, N // P], F32, name="bias")
+        with nc.allow_non_contiguous_dma(reason="one bias value a partition"):
+            nc.gpsimd.dma_start(bias[:], b.rearrange("(m p) -> p m", p=P))
 
-        wd_raw = stage.tile([P, SLOTS, N], F32, name="wd_raw", offset=4 * R + CHUNK, align_bytes=64)
-        wd_rows = wd.rearrange("(q s i) n -> i q s n", s=SLOTS, i=RUN)
-        for i in [x + half for x in range(RUN // 2) for half in (0, RUN // 2)]:
-            nc.sync.dma_start(wd_raw[i:P:RUN, :, :], wd_rows[i])
+        planes.append(stage.tile([P, LISTS * CHUNK // 4], I32, name="plane1", offset=4 * R, align_bytes=64))
+        wd_raw = stage.tile([P, SLOTS, N], F32, name="wd_raw", offset=5 * R + CHUNK, align_bytes=64)
+        wd_rows = wd.rearrange("(q s i) n -> s q (i n)", s=SLOTS, i=RUN)
+        for s in range(SLOTS):
+            nc.sync.dma_start(wd_raw[:, s, :], wd_rows[s])
+        move_scales(1, picked_sc1a, (0, 1))
 
-        picked_sc1 = stage.tile([P, 2 * CHUNK], U8, name="picked_sc1", offset=2 * R, align_bytes=64)
-        move_scales(1, picked_sc10, (0,))
-        gather_scales(1, picked_sc1, (1, 2))
-        move_scales(1, picked_sc1, (1, 2))
+        picked_sc1b = stage.tile([P, CHUNK], U8, name="picked_sc1b", offset=2 * R, align_bytes=64)
+        gather_scales(1, picked_sc1b, (2,))
+        move_scales(1, picked_sc1b, (2,))
         picked1 = keep.tile([P, LISTS, CHUNK], U32, name="picked1", tag="table_sc", align_bytes=64)
         for g in range(LISTS):
             picked_words[1, g] = gather_words(1, g, picked1[:, g, :])
@@ -156,23 +153,30 @@ def tile_list_rvq_gelu_gelu_kernel(
         all_acts = []
 
         def scale_in_pairs(c, a, j_first, width, weaver):
-            scaled = keep.tile([P, PACK // 2, width, 2], BF16, name=f"scaled{c}_{a}", tag=f"scaled{c}_{a}", align_bytes=64)
+            scaled = keep.tile([P, PACK, width], BF16, name=f"scaled{c}_{a}", tag=f"scaled{c}_{a}", align_bytes=64)
             woven = keep.tile([P, width, PACK], BF16, name=f"woven{c}_{a}", tag=f"woven{c}_{a}", align_bytes=64)
             for t in range(PACK):
                 s = a * PACK + t
                 nc.gpsimd.tensor_scalar(
-                    scaled[:, t // 2, :, t % 2],
+                    scaled[:, t, :],
                     all_acts[c][a][:, t, j_first : j_first + width],
                     cols[:, s : s + 1],
                     0.0,
                     MULT,
                     ADD,
                 )
-            weaver(woven[:].bitcast(U32), scaled[:].bitcast(U32).rearrange("p u j x -> p j (u x)"))
+            for j0 in range(0, width, PIECE):
+                weaver(
+                    woven[:, j0 : j0 + PIECE, :].rearrange("p (z e) t -> p z t e", e=4),
+                    scaled[:, :, j0 : j0 + PIECE].rearrange("p t (z e) -> p z t e", e=4),
+                )
             return woven
 
         def scale_on_vector(c, a, j_first, width):
-            woven = keep.tile([P, width, PACK], BF16, name=f"h{c}_{a}_{j_first}", tag=("scaled0_1", "act1_0")[a], align_bytes=64)
+            if c == 0:
+                woven = stage.tile([P, width, PACK], BF16, name="h0_0", offset=20 * R, align_bytes=64)
+            else:
+                woven = keep.tile([P, width, PACK], BF16, name=f"h1_{a}", tag=("act0_0", "act1_0")[a], align_bytes=64)
             factor = turned[:, a * PACK : (a + 1) * PACK].unsqueeze(1).unsqueeze(3)
             nc.vector.tensor_tensor(
                 woven[:].rearrange("p (z e) t -> p z t e", e=2),
@@ -183,8 +187,8 @@ def tile_list_rvq_gelu_gelu_kernel(
             return woven
 
         def quantise(name, values, width, tag=None):
-            if name == "h0_0":
-                codes = stage.tile([P, width], U32, name="h0_0_codes", offset=6 * R, align_bytes=64)
+            if tag == "wd":
+                codes = stage.tile([P, width], U32, name="wd_codes", offset=24 * R, align_bytes=64)
             else:
                 codes = keep.tile([P, width], U32, name=f"{name}_codes", tag=tag or f"{name}_codes", align_bytes=64)
             plane = keep.tile([P, width], U8, name=f"{name}_sc", align_bytes=64)
@@ -213,12 +217,13 @@ def tile_list_rvq_gelu_gelu_kernel(
                 if g == LISTS - 1:
                     nc.scalar.activation(acts[s // PACK][:, s % PACK, :], accs[s][:], GELU)
             if c == 0:
-                woven0.append(scale_in_pairs(0, 0, 0, CHUNK, nc.scalar.copy))
-                wd_bf = keep.tile([P, PASSES, N, PACK], BF16, name="wd_bf", tag="woven0_1", align_bytes=64)
+                wd_bf = stage.tile([P, PASSES, N, PACK], BF16, name="wd_bf", offset=16 * R, align_bytes=64)
                 for a in range(PASSES):
-                    nc.vector.tensor_copy(wd_bf[:, a], wd_raw[:, a * PACK : (a + 1) * PACK, :].rearrange("p t n -> p n t"))
+                    wd_pass = wd_raw[:, a * PACK : (a + 1) * PACK, :].rearrange("p t n -> p n t")
+                    nc.gpsimd.tensor_scalar(wd_bf[:, a], wd_pass, 1.0, 0.0, MULT, ADD)
                 flat = "p j t -> p (j t)"
-                wd_codes, wd_sc = quantise("wd", wd_bf[:].rearrange("p a n t -> p (a n t)"), PASSES * N)
+                woven0.append(scale_on_vector(0, 0, 0, CHUNK))
+                wd_codes, wd_sc = quantise("wd", wd_bf[:].rearrange("p a n t -> p (a n t)"), PASSES * N, "wd")
                 woven0.append(scale_in_pairs(0, 1, 0, CHUNK, nc.vector.tensor_copy))
 
         h0 = [quantise(f"h0_{a}", woven0[a][:].rearrange(flat), CHUNK) for a in range(PASSES)]

@@ -31,7 +31,7 @@ BANKS = 7
 CHUNK = 512
 PIECE = 256
 GPSIMD_ZEROED = 5 * T // 32
-AHEAD = (2, 4)
+AHEAD = (2, 0)
 COLS = 8
 
 
@@ -65,12 +65,13 @@ def tile_list_rvq_gelu_gelu_kernel(
             nc.sync.dma_start(sc_raw[:, g, :], w_scales[g][0].bitcast(I32))
 
         def load_words(g):
-            raw = stage.tile([P, R // 2], I32, name=f"w_raw{g}", offset=(0, 4 * R - 64, 2 * R)[g], align_bytes=64)
+            raw = stage.tile([P, R // 2], I32, name=f"w_raw{g}", offset=(4 * R - 64, 0, 2 * R)[g], align_bytes=64)
             nc.sync.dma_start(raw[:], w_words[g][0].bitcast(I32))
             return raw
 
-        w_raw = [load_words(0), load_words(1)]
+        w_raw = [load_words(0)]
         nc.sync.dma_start(table[:], tab_words[0].rearrange("p t i -> p (t i)").bitcast(I32))
+        w_raw.append(load_words(1))
 
         ident = keep.tile([P, P], F32, name="ident")
         make_identity(nc, ident[:])
@@ -117,7 +118,7 @@ def tile_list_rvq_gelu_gelu_kernel(
         gather_scales(0, picked_sc0, (0, 1, 2))
         move_scales(0, picked_sc0, (0, 1, 2))
         for quad in range(1, QUADS):
-            nc.sync.dma_start(w_sc[32 * quad : 32 * quad + 4, :], w_sc[4 * quad : 4 * quad + 4, :])
+            (nc.gpsimd if quad == 1 else nc.sync).dma_start(w_sc[32 * quad : 32 * quad + 4, :], w_sc[4 * quad : 4 * quad + 4, :])
         w_ord = [order_words(0), order_words(1)]
         w_raw.append(load_words(2))
         picked_sc1a = keep.tile([P, 2 * CHUNK], U8, name="picked_sc1a", align_bytes=64)
@@ -126,7 +127,7 @@ def tile_list_rvq_gelu_gelu_kernel(
         picked0 = keep.tile([P, LISTS, CHUNK], U32, name="picked0", align_bytes=64)
         for g in range(LISTS):
             picked_words[0, g] = gather_words(0, g, picked0[:, g, :])
-        cols = keep.tile([P, COLS], F32, name="cols")
+        cols = stage.tile([P, COLS], F32, name="cols", offset=0)
         nc.vector.tensor_copy(cols[:], turned[:, 0:COLS])
         w_ord.append(order_words(2))
         bias = keep.tile([P, N // P], F32, name="bias")
@@ -166,33 +167,41 @@ def tile_list_rvq_gelu_gelu_kernel(
                     ADD,
                 )
             for j0 in range(0, width, PIECE):
-                weaver(
+                weaver[j0 // PIECE](
                     woven[:, j0 : j0 + PIECE, :].rearrange("p (z e) t -> p z t e", e=4),
                     scaled[:, :, j0 : j0 + PIECE].rearrange("p t (z e) -> p z t e", e=4),
                 )
             return woven
 
-        def scale_on_vector(c, a, j_first, width):
+        def scale_on_vector(c, a, j_first, width, parts=1):
             if c == 0:
                 woven = stage.tile([P, width, PACK], BF16, name="h0_0", offset=20 * R, align_bytes=64)
             else:
-                woven = keep.tile([P, width, PACK], BF16, name=f"h1_{a}", tag=("act0_0", "act1_0")[a], align_bytes=64)
+                woven = keep.tile([P, width, PACK], BF16, name=f"h1_{a}_{j_first}", tag=("act0_0", "act1_0", "scaled0_1")[a + j_first // P], align_bytes=64)
             factor = turned[:, a * PACK : (a + 1) * PACK].unsqueeze(1).unsqueeze(3)
-            nc.vector.tensor_tensor(
-                woven[:].rearrange("p (z e) t -> p z t e", e=2),
-                all_acts[c][a][:, :, j_first : j_first + width].rearrange("p t (z e) -> p z t e", e=2),
-                factor.to_broadcast([P, width // 2, PACK, 2]),
-                MULT,
-            )
+            step = width // parts
+            for j0 in range(0, width, step):
+                nc.vector.tensor_tensor(
+                    woven[:, j0 : j0 + step, :].rearrange("p (z e) t -> p z t e", e=2),
+                    all_acts[c][a][:, :, j_first + j0 : j_first + j0 + step].rearrange("p t (z e) -> p z t e", e=2),
+                    factor.to_broadcast([P, step // 2, PACK, 2]),
+                    MULT,
+                )
             return woven
 
-        def quantise(name, values, width, tag=None):
+        def quantise(name, values, width, tag=None, parts=1):
             if tag == "wd":
                 codes = stage.tile([P, width], U32, name="wd_codes", offset=24 * R, align_bytes=64)
             else:
                 codes = keep.tile([P, width], U32, name=f"{name}_codes", tag=tag or f"{name}_codes", align_bytes=64)
             plane = keep.tile([P, width], U8, name=f"{name}_sc", align_bytes=64)
-            nc.vector.quantize_mx(out=codes[:].bitcast(FP8X4), scales=plane[:], in_=values)
+            step = width // parts
+            for j0 in range(0, width, step):
+                nc.vector.quantize_mx(
+                    out=codes[:, j0 : j0 + step].bitcast(FP8X4),
+                    scales=plane[:, j0 : j0 + step],
+                    in_=values[:, PACK * j0 : PACK * (j0 + step)],
+                )
             return codes, plane
 
         woven0 = []
@@ -215,7 +224,9 @@ def tile_list_rvq_gelu_gelu_kernel(
                     stop=(g == LISTS - 1),
                 )
                 if g == LISTS - 1:
-                    nc.scalar.activation(acts[s // PACK][:, s % PACK, :], accs[s][:], GELU)
+                    step = PIECE if (c, s) == (chunks - 1, SLOTS - 1) else CHUNK
+                    for j0 in range(0, CHUNK, step):
+                        nc.scalar.activation(acts[s // PACK][:, s % PACK, j0 : j0 + step], accs[s][:, j0 : j0 + step], GELU)
             if c == 0:
                 wd_bf = stage.tile([P, PASSES, N, PACK], BF16, name="wd_bf", offset=16 * R, align_bytes=64)
                 for a in range(PASSES):
@@ -224,18 +235,20 @@ def tile_list_rvq_gelu_gelu_kernel(
                 flat = "p j t -> p (j t)"
                 woven0.append(scale_on_vector(0, 0, 0, CHUNK))
                 wd_codes, wd_sc = quantise("wd", wd_bf[:].rearrange("p a n t -> p (a n t)"), PASSES * N, "wd")
-                woven0.append(scale_in_pairs(0, 1, 0, CHUNK, nc.vector.tensor_copy))
+                woven0.append(scale_in_pairs(0, 1, 0, CHUNK, [nc.vector.tensor_copy, nc.vector.tensor_copy]))
 
-        h0 = [quantise(f"h0_{a}", woven0[a][:].rearrange(flat), CHUNK) for a in range(PASSES)]
-        woven10 = scale_on_vector(1, 0, 0, CHUNK)
-        h10 = quantise("h1_0", woven10[:].rearrange(flat), CHUNK)
-        last_woven = scale_in_pairs(1, 1, PIECE, PIECE, nc.scalar.copy)
-        h11 = [quantise("h1_1a", scale_on_vector(1, 1, 0, PIECE)[:].rearrange(flat), PIECE)]
-        h11.append(quantise("h1_1b", last_woven[:].rearrange(flat), PIECE, "act1_1"))
+        h0 = [quantise(f"h0_{a}", woven0[a][:].rearrange(flat), CHUNK, None, 1 + a) for a in range(PASSES)]
+        woven10 = [scale_on_vector(1, 0, half * PIECE, PIECE) for half in range(2)]
+        h10 = [quantise(f"h1_0{half}", woven10[half][:].rearrange(flat), PIECE) for half in range(2)]
+        h11 = [quantise("h1_1a", scale_on_vector(1, 1, 0, PIECE, 2)[:].rearrange(flat), PIECE, None, 2)]
+        last_woven = scale_in_pairs(1, 1, PIECE, PIECE, [nc.scalar.copy])
+        h11.append(quantise("h1_1b", last_woven[:].rearrange(flat), PIECE))
 
-        def second_layer(j0, width, operands, follows):
-            ybanks = [psum.tile([P, width], F32, name=f"y{j0}_{m}", tag=bank_of(1, follows[m])) for m in range(N // P)]
-            for a in range(PASSES):
+        def open_banks(j0, width, follows):
+            return [psum.tile([P, width], F32, name=f"y{j0}_{m}", tag=bank_of(1, follows[m])) for m in range(N // P)]
+
+        def second_layer(j0, width, operands, ybanks, passes):
+            for a in passes:
                 for m in range(N // P):
                     first = a * N + m * P
                     nc.tensor.matmul_mx(
@@ -247,13 +260,16 @@ def tile_list_rvq_gelu_gelu_kernel(
                         start=(a == 0),
                         stop=(a == PASSES - 1),
                     )
-            for m in range(N // P):
-                result = keep.tile([P, width], F32, name=f"result{j0}_{m}")
+            for m in range(N // P if PASSES - 1 in passes else 0):
+                tag = f"result{j0}_{m}"
+                result = keep.tile([P, width], F32, name=f"result{j0}_{m}", tag=tag, align_bytes=64)
                 nc.scalar.activation(result[:], ybanks[m][:], GELU, bias=bias[:, m : m + 1])
                 nc.sync.dma_start(out[m * P : (m + 1) * P, j0 : j0 + width], result[:])
 
-        second_layer(0, CHUNK, [(codes[:], plane[:]) for codes, plane in h0], (5, 6))
-        for half in range(CHUNK // PIECE):
-            js = slice(half * PIECE, (half + 1) * PIECE)
-            operands = [(h10[0][:, js], h10[1][:, js]), (h11[half][0][:], h11[half][1][:])]
-            second_layer(CHUNK + half * PIECE, PIECE, operands, (1 + 2 * half, 2 + 2 * half))
+        second_layer(0, CHUNK, [(codes[:], plane[:]) for codes, plane in h0], open_banks(0, CHUNK, (5, 6)), (0, 1))
+        halves = range(CHUNK // PIECE)
+        last_banks = [open_banks(CHUNK + half * PIECE, PIECE, (1 + 2 * half, 2 + 2 * half)) for half in halves]
+        for a in range(PASSES):
+            for half in halves:
+                operands = [(h10[half][0][:], h10[half][1][:]), (h11[half][0][:], h11[half][1][:])]
+                second_layer(CHUNK + half * PIECE, PIECE, operands, last_banks[half], (a,))

@@ -121,8 +121,8 @@ def tile_list_rvq_gelu_gelu_kernel(
             (nc.gpsimd if quad == 1 else nc.sync).dma_start(w_sc[32 * quad : 32 * quad + 4, :], w_sc[4 * quad : 4 * quad + 4, :])
         w_ord = [order_words(0), order_words(1)]
         w_raw.append(load_words(2))
-        picked_sc1a = keep.tile([P, 2 * CHUNK], U8, name="picked_sc1a", align_bytes=64)
-        gather_scales(1, picked_sc1a, (0, 1))
+        picked_sc1a = keep.tile([P, CHUNK], U8, name="picked_sc1a", align_bytes=64)
+        gather_scales(1, picked_sc1a, (0,))
         picked_words = {}
         picked0 = keep.tile([P, LISTS, CHUNK], U32, name="picked0", align_bytes=64)
         for g in range(LISTS):
@@ -139,11 +139,11 @@ def tile_list_rvq_gelu_gelu_kernel(
         wd_rows = wd.rearrange("(q s i) n -> s q (i n)", s=SLOTS, i=RUN)
         for s in range(SLOTS):
             nc.sync.dma_start(wd_raw[:, s, :], wd_rows[s])
-        move_scales(1, picked_sc1a, (0, 1))
+        move_scales(1, picked_sc1a, (0,))
 
-        picked_sc1b = stage.tile([P, CHUNK], U8, name="picked_sc1b", offset=2 * R, align_bytes=64)
-        gather_scales(1, picked_sc1b, (2,))
-        move_scales(1, picked_sc1b, (2,))
+        picked_sc1b = stage.tile([P, 2 * CHUNK], U8, name="picked_sc1b", offset=2 * R, align_bytes=64)
+        gather_scales(1, picked_sc1b, (1, 2))
+        move_scales(1, picked_sc1b, (1, 2))
         picked1 = keep.tile([P, LISTS, CHUNK], U32, name="picked1", tag="table_sc", align_bytes=64)
         for g in range(LISTS):
             picked_words[1, g] = gather_words(1, g, picked1[:, g, :])

@@ -177,7 +177,7 @@ def tile_list_rvq_gelu_gelu_kernel(
             if c == 0:
                 woven = stage.tile([P, width, PACK], BF16, name="h0_0", offset=20 * R, align_bytes=64)
             else:
-                woven = keep.tile([P, width, PACK], BF16, name=f"h1_{a}_{j_first}", tag=("act0_0", "act1_0", "scaled0_1")[a + j_first // P], align_bytes=64)
+                woven = keep.tile([P, width, PACK], BF16, name=f"h1_{a}_{j_first}", tag=("act0_0", "act1_0", "act0_1")[a + j_first // P], align_bytes=64)
             factor = turned[:, a * PACK : (a + 1) * PACK].unsqueeze(1).unsqueeze(3)
             step = width // parts
             for j0 in range(0, width, step):
@@ -189,19 +189,26 @@ def tile_list_rvq_gelu_gelu_kernel(
                 )
             return woven
 
-        def quantise(name, values, width, tag=None, parts=1):
+        def quantise(name, values, width, tag=None, parts=1, later=None):
             if tag == "wd":
                 codes = stage.tile([P, width], U32, name="wd_codes", offset=24 * R, align_bytes=64)
             else:
                 codes = keep.tile([P, width], U32, name=f"{name}_codes", tag=tag or f"{name}_codes", align_bytes=64)
             plane = keep.tile([P, width], U8, name=f"{name}_sc", align_bytes=64)
             step = width // parts
-            for j0 in range(0, width, step):
+
+            def part(j0):
                 nc.vector.quantize_mx(
                     out=codes[:, j0 : j0 + step].bitcast(FP8X4),
                     scales=plane[:, j0 : j0 + step],
                     in_=values[:, PACK * j0 : PACK * (j0 + step)],
                 )
+
+            for j0 in range(0, width, step):
+                if later is not None and j0 > 0:
+                    later.append(lambda: part(step))
+                else:
+                    part(j0)
             return codes, plane
 
         woven0 = []
@@ -235,10 +242,12 @@ def tile_list_rvq_gelu_gelu_kernel(
                 flat = "p j t -> p (j t)"
                 woven0.append(scale_on_vector(0, 0, 0, CHUNK))
                 wd_codes, wd_sc = quantise("wd", wd_bf[:].rearrange("p a n t -> p (a n t)"), PASSES * N, "wd")
-                woven0.append(scale_in_pairs(0, 1, 0, CHUNK, [nc.vector.tensor_copy, nc.vector.tensor_copy]))
+                woven0.append(scale_in_pairs(0, 1, 0, CHUNK, [nc.vector.tensor_copy, nc.scalar.copy]))
 
-        h0 = [quantise(f"h0_{a}", woven0[a][:].rearrange(flat), CHUNK, None, 1 + a) for a in range(PASSES)]
+        later = []
+        h0 = [quantise(f"h0_{a}", woven0[a][:].rearrange(flat), CHUNK, None, 1 + a, later) for a in range(PASSES)]
         woven10 = [scale_on_vector(1, 0, half * PIECE, PIECE) for half in range(2)]
+        later[0]()
         h10 = [quantise(f"h1_0{half}", woven10[half][:].rearrange(flat), PIECE) for half in range(2)]
         h11 = [quantise("h1_1a", scale_on_vector(1, 1, 0, PIECE, 2)[:].rearrange(flat), PIECE, None, 2)]
         last_woven = scale_in_pairs(1, 1, PIECE, PIECE, [nc.scalar.copy])

@@ -97,7 +97,7 @@ def tile_list_rvq_gelu_gelu_kernel(
             columns = slice(lists[0] * CHUNK // 4, (lists[-1] + 1) * CHUNK // 4)
             for quad in range(QUADS):
                 first = P - SCALE_ROWS + 4 * quad
-                nc.sync.dma_start(
+                (nc.scalar if c == 0 else nc.sync).dma_start(
                     planes[c][32 * quad : 32 * quad + 4, columns], picked_sc[:].bitcast(I32)[first : first + 4, :]
                 )
 

@@ -31,7 +31,7 @@ BANKS = 7
 CHUNK = 512
 PIECE = 256
 GPSIMD_ZEROED = 5 * T // 32
-AHEAD = (2, 0)
+AHEAD = (4, 0)
 COLS = 8
 
 
@@ -70,7 +70,9 @@ def tile_list_rvq_gelu_gelu_kernel(
             return raw
 
         w_raw = [load_words(0)]
-        nc.sync.dma_start(table[:], tab_words[0].rearrange("p t i -> p (t i)").bitcast(I32))
+        table_rows = tab_words[0].rearrange("p t i -> p (t i)").bitcast(I32)
+        for half in range(2):
+            nc.sync.dma_start(table[:, half * T // 2 : (half + 1) * T // 2], table_rows[:, half * T // 2 : (half + 1) * T // 2])
         w_raw.append(load_words(1))
 
         ident = keep.tile([P, P], F32, name="ident")
@@ -121,6 +123,17 @@ def tile_list_rvq_gelu_gelu_kernel(
             (nc.gpsimd if quad == 1 else nc.sync).dma_start(w_sc[32 * quad : 32 * quad + 4, :], w_sc[4 * quad : 4 * quad + 4, :])
         w_ord = [order_words(0), order_words(1)]
         w_raw.append(load_words(2))
+        warm = psum.tile([P, CHUNK], F32, name="warm", tag="bank6")
+        for n in range(4):
+            nc.tensor.matmul_mx(
+                out=warm[:],
+                lhsT=w_ord[0][:].bitcast(U8)[:, 0 : 2 * P].bitcast(FP4X4),
+                lhsT_scale=table_sc[:].bitcast(U8)[:, 0:P],
+                rhs=table[:, n * CHUNK : (n + 1) * CHUNK].bitcast(FP8X4),
+                rhs_scale=table_sc[:].bitcast(U8)[:, 0:CHUNK],
+                start=True,
+                stop=True,
+            )
         picked_sc1a = keep.tile([P, CHUNK], U8, name="picked_sc1a", align_bytes=64)
         gather_scales(1, picked_sc1a, (0,))
         picked_words = {}
@@ -152,6 +165,9 @@ def tile_list_rvq_gelu_gelu_kernel(
             return f"bank{(c * SLOTS + s) % BANKS}"
 
         all_acts = []
+
+        def weave_on_gpsimd(dst, values):
+            nc.gpsimd.tensor_scalar(dst.rearrange("p z t e -> p z e t"), values.rearrange("p z t e -> p z e t"), 1.0, 0.0, MULT, ADD)
 
         def scale_in_pairs(c, a, j_first, width, weaver):
             scaled = keep.tile([P, PACK, width], BF16, name=f"scaled{c}_{a}", tag=f"scaled{c}_{a}", align_bytes=64)
@@ -242,7 +258,7 @@ def tile_list_rvq_gelu_gelu_kernel(
                 flat = "p j t -> p (j t)"
                 woven0.append(scale_on_vector(0, 0, 0, CHUNK))
                 wd_codes, wd_sc = quantise("wd", wd_bf[:].rearrange("p a n t -> p (a n t)"), PASSES * N, "wd")
-                woven0.append(scale_in_pairs(0, 1, 0, CHUNK, [nc.vector.tensor_copy, nc.scalar.copy]))
+                woven0.append(scale_in_pairs(0, 1, 0, CHUNK, [weave_on_gpsimd, nc.scalar.copy]))
 
         later = []
         h0 = [quantise(f"h0_{a}", woven0[a][:].rearrange(flat), CHUNK, None, 1 + a, later) for a in range(PASSES)]

@@ -109,7 +109,7 @@ def tile_list_rvq_gelu_gelu_kernel(
 
         def order_words(g):
             ordered = keep.tile([P, R // 2], I32, name=f"w_ord{g}", align_bytes=64)
-            nc.gpsimd.tensor_copy(
+            (nc.vector if g == 2 else nc.gpsimd).tensor_copy(
                 ordered[:].rearrange("p (s q x) -> p s q x", s=SLOTS, x=4),
                 w_raw[g][:].rearrange("p (q s x) -> p s q x", s=SLOTS, x=4),
             )

@@ -124,13 +124,13 @@ def tile_list_rvq_gelu_gelu_kernel(
         w_ord = [order_words(0), order_words(1)]
         w_raw.append(load_words(2))
         warm = psum.tile([P, CHUNK], F32, name="warm", tag="bank6")
-        for n in range(4):
+        for n in range(5):
             nc.tensor.matmul_mx(
                 out=warm[:],
-                lhsT=w_ord[0][:].bitcast(U8)[:, 0 : 2 * P].bitcast(FP4X4),
+                lhsT=table[:, 0 : P // 2].bitcast(U8).bitcast(FP4X4),
                 lhsT_scale=table_sc[:].bitcast(U8)[:, 0:P],
-                rhs=table[:, n * CHUNK : (n + 1) * CHUNK].bitcast(FP8X4),
-                rhs_scale=table_sc[:].bitcast(U8)[:, 0:CHUNK],
+                rhs=table[:, 0:CHUNK].bitcast(FP8X4),
+                rhs_scale=picked_sc0[:, 2 * CHUNK : 3 * CHUNK],
                 start=True,
                 stop=True,
             )

@@ -65,8 +65,8 @@ def tile_list_rvq_gelu_gelu_kernel(
             nc.sync.dma_start(sc_raw[:, g, :], w_scales[g][0].bitcast(I32))
 
         def load_words(g):
-            raw = stage.tile([P, R // 2], I32, name=f"w_raw{g}", offset=(4 * R - 64, 0, 2 * R)[g], align_bytes=64)
-            nc.sync.dma_start(raw[:], w_words[g][0].bitcast(I32))
+            raw = stage.tile([P, R // 2], I32, name=f"w_raw{g}", offset=(36 * R, 4 * R, 36 * R)[g], align_bytes=64)
+            (nc.scalar if g == 2 else nc.sync).dma_start(raw[:], w_words[g][0].bitcast(I32))
             return raw
 
         w_raw = [load_words(0)]
@@ -120,7 +120,7 @@ def tile_list_rvq_gelu_gelu_kernel(
         gather_scales(0, picked_sc0, (0, 1, 2))
         move_scales(0, picked_sc0, (0, 1, 2))
         for quad in range(1, QUADS):
-            (nc.gpsimd if quad == 1 else nc.sync).dma_start(w_sc[32 * quad : 32 * quad + 4, :], w_sc[4 * quad : 4 * quad + 4, :])
+            (nc.gpsimd if quad == 1 else nc.scalar).dma_start(w_sc[32 * quad : 32 * quad + 4, :], w_sc[4 * quad : 4 * quad + 4, :])
         w_ord = [order_words(0), order_words(1)]
         w_raw.append(load_words(2))
         warm = psum.tile([P, CHUNK], F32, name="warm", tag="bank6")
@@ -140,7 +140,7 @@ def tile_list_rvq_gelu_gelu_kernel(
         picked0 = keep.tile([P, LISTS, CHUNK], U32, name="picked0", align_bytes=64)
         for g in range(LISTS):
             picked_words[0, g] = gather_words(0, g, picked0[:, g, :])
-        cols = stage.tile([P, COLS], F32, name="cols", offset=0)
+        cols = stage.tile([P, COLS], F32, name="cols", offset=37 * R)
         nc.vector.tensor_copy(cols[:], turned[:, 0:COLS])
         w_ord.append(order_words(2))
         bias = keep.tile([P, N // P], F32, name="bias")
@@ -154,7 +154,7 @@ def tile_list_rvq_gelu_gelu_kernel(
             nc.sync.dma_start(wd_raw[:, s, :], wd_rows[s])
         move_scales(1, picked_sc1a, (0,))
 
-        picked_sc1b = stage.tile([P, 2 * CHUNK], U8, name="picked_sc1b", offset=2 * R, align_bytes=64)
+        picked_sc1b = stage.tile([P, 2 * CHUNK], U8, name="picked_sc1b", offset=36 * R, align_bytes=64)
         gather_scales(1, picked_sc1b, (1, 2))
         move_scales(1, picked_sc1b, (1, 2))
         picked1 = keep.tile([P, LISTS, CHUNK], U32, name="picked1", tag="table_sc", align_bytes=64)

@@ -30,9 +30,10 @@ SLOTS = PASSES * PACK
 BANKS = 7
 CHUNK = 512
 PIECE = 256
-GPSIMD_ZEROED = 5 * T // 32
-AHEAD = (4, 0)
+AHEAD = (4, 4)
+WARM_UPS = 5
 COLS = 8
+KB = 1024
 
 
 def tile_list_rvq_gelu_gelu_kernel(
@@ -48,118 +49,110 @@ def tile_list_rvq_gelu_gelu_kernel(
         stage = ctx.enter_context(tc.tile_pool(name="stage", bufs=1))
         psum = ctx.enter_context(tc.psum_pool(name="psum", bufs=1))
 
+        def placed(name, shape, dtype, offset):
+            return stage.tile(shape, dtype, name=name, offset=offset, align_bytes=64)
+
         offsets = keep.tile([P, LISTS * J // GROUP], U16, name="offsets")
-        table = stage.tile([P, T], I32, name="table", offset=20 * R, align_bytes=64)
+        table = placed("table", [P, T], I32, 0)
         table_sc = keep.tile([P, T // 4], I32, name="table_sc", tag="table_sc", align_bytes=64)
         nc.sync.dma_start(offsets[:], offs)
         nc.sync.dma_start(table_sc[P - SCALE_ROWS : P, :], tab_scales[0].bitcast(I32))
-        rows = keep.tile([P, P], F32, name="rows", align_bytes=64)
-        nc.gpsimd.memset(rows[:], 0.0)
-        nc.gpsimd.dma_start(
-            rows[0:SLOTS, :].rearrange("s (q i) -> s q i", i=RUN), sm.rearrange("(q s i) -> s q i", s=SLOTS, i=RUN)
-        )
+        seed = placed("seed", [P, P], F32, 40 * KB)
+        nc.vector.memset(seed[:], 0.0)
         nc.vector.memset(table_sc[0 : P - SCALE_ROWS, :], 0)
-        w_sc = keep.tile([P, LISTS * R // 4], I32, name="w_sc", align_bytes=64)
-        sc_raw = keep.tile([SCALE_ROWS, LISTS, R // 4], I32, name="sc_raw", align_bytes=64)
+        sc_raw = placed("sc_raw", [SCALE_ROWS, LISTS * R // 4], I32, 16 * KB)
         for g in range(LISTS):
-            nc.sync.dma_start(sc_raw[:, g, :], w_scales[g][0].bitcast(I32))
-
-        def load_words(g):
-            raw = stage.tile([P, R // 2], I32, name=f"w_raw{g}", offset=(36 * R, 4 * R, 36 * R)[g], align_bytes=64)
-            (nc.scalar if g == 2 else nc.sync).dma_start(raw[:], w_words[g][0].bitcast(I32))
-            return raw
-
-        w_raw = [load_words(0)]
+            nc.sync.dma_start(sc_raw[:, g * R // 4 : (g + 1) * R // 4], w_scales[g][0].bitcast(I32))
         table_rows = tab_words[0].rearrange("p t i -> p (t i)").bitcast(I32)
         for half in range(2):
-            nc.sync.dma_start(table[:, half * T // 2 : (half + 1) * T // 2], table_rows[:, half * T // 2 : (half + 1) * T // 2])
-        w_raw.append(load_words(1))
+            columns = slice(half * T // 2, (half + 1) * T // 2)
+            nc.sync.dma_start(table[:, columns], table_rows[:, columns])
+        w_raw = [placed(f"w_raw{g}", [P, R // 2], I32, (20, 24, 22)[g] * KB) for g in range(LISTS)]
+        for g in range(LISTS):
+            nc.sync.dma_start(w_raw[g][:], w_words[g][0].bitcast(I32))
 
         ident = keep.tile([P, P], F32, name="ident")
         make_identity(nc, ident[:])
-        turned = psum.tile([P, CHUNK], F32, name="turned", tag="vectors")
-        nc.tensor.transpose(turned[:, 0:P], rows[:], ident[:])
-
-        nc.gpsimd.tensor_copy(
-            w_sc[0:SCALE_ROWS, :].rearrange("p (g s q x) -> p g s q x", g=LISTS, s=SLOTS, x=2),
-            sc_raw[:].rearrange("p g (q s x) -> p g s q x", s=SLOTS, x=2),
+        rows = keep.tile([P, PASSES, P], F32, name="rows", align_bytes=64)
+        nc.scalar.activation(rows[:], seed[:].unsqueeze(1).to_broadcast([P, PASSES, P]), GELU)
+        nc.gpsimd.dma_start(
+            rows[0:PACK].rearrange("t a (q i) -> t (a q) i", i=RUN), sm.rearrange("(z t i) -> t z i", t=PACK, i=RUN)
         )
+        turned = psum.tile([P, PASSES, P], F32, name="turned", tag="vectors")
+        for a in range(PASSES):
+            nc.tensor.transpose(turned[:, a, :], rows[:, a, :], ident[:])
+
+        w_sc = placed("w_sc", [P, LISTS * R // 4], I32, 40 * KB)
+        nc.scalar.copy(
+            w_sc[0:SCALE_ROWS, :].bitcast(U32).rearrange("p (z t q x) -> p z t q x", t=PACK, q=SCALE_ROWS, x=2),
+            sc_raw[:].bitcast(U32).rearrange("p (z q t x) -> p z t q x", t=PACK, q=SCALE_ROWS, x=2),
+        )
+        for quad in range(1, QUADS):
+            nc.gpsimd.dma_start(w_sc[32 * quad : 32 * quad + 4, :], w_sc[4 * quad : 4 * quad + 4, :])
 
         def list_slice(c, g):
             column = (g * J + c * CHUNK) // GROUP
             return offsets[:, column : column + CHUNK // GROUP]
 
-        def gather_scales(c, picked_sc, lists):
-            for n, g in enumerate(lists):
-                nc.vector.tensor_copy(
-                    picked_sc[:, n * CHUNK : (n + 1) * CHUNK], table_sc[:].bitcast(U8).indirect(list_slice(c, g))
-                )
+        plane_of = {}
 
-        def move_scales(c, picked_sc, lists):
-            columns = slice(lists[0] * CHUNK // 4, (lists[-1] + 1) * CHUNK // 4)
+        def scale_batch(name, members, picked_at, plane_at, queue):
+            picked = placed(f"picked_{name}", [P, len(members) * CHUNK], U8, picked_at)
+            plane = placed(f"plane_{name}", [P, len(members) * CHUNK // 4], I32, plane_at)
+            for n, (c, g) in enumerate(members):
+                nc.vector.tensor_copy(
+                    picked[:, n * CHUNK : (n + 1) * CHUNK], table_sc[:].bitcast(U8).indirect(list_slice(c, g))
+                )
+                plane_of[c, g] = plane[:].bitcast(U8)[:, n * CHUNK : (n + 1) * CHUNK]
             for quad in range(QUADS):
                 first = P - SCALE_ROWS + 4 * quad
-                (nc.scalar if c == 0 else nc.sync).dma_start(
-                    planes[c][32 * quad : 32 * quad + 4, columns], picked_sc[:].bitcast(I32)[first : first + 4, :]
-                )
-
-        def gather_words(c, g, picked):
-            nc.vector.tensor_copy(picked, table[:].bitcast(U32).indirect(list_slice(c, g)))
+                queue.dma_start(plane[32 * quad : 32 * quad + 4, :], picked[:].bitcast(I32)[first : first + 4, :])
             return picked
 
-        def order_words(g):
-            ordered = keep.tile([P, R // 2], I32, name=f"w_ord{g}", align_bytes=64)
-            (nc.vector if g == 2 else nc.gpsimd).tensor_copy(
-                ordered[:].rearrange("p (s q x) -> p s q x", s=SLOTS, x=4),
-                w_raw[g][:].rearrange("p (q s x) -> p s q x", s=SLOTS, x=4),
-            )
-            return ordered
+        scale_batch("a", ((0, 0), (0, 1)), 19 * KB, 16 * KB, nc.scalar)
+        picked_b = scale_batch("b", ((0, 2), (1, 0)), 34 * KB, 19 * KB, nc.sync)
 
-        planes = [keep.tile([P, LISTS * CHUNK // 4], I32, name="plane0", align_bytes=64)]
-        picked_sc0 = keep.tile([P, LISTS * CHUNK], U8, name="picked_sc0", align_bytes=64)
-        gather_scales(0, picked_sc0, (0, 1, 2))
-        move_scales(0, picked_sc0, (0, 1, 2))
-        for quad in range(1, QUADS):
-            (nc.gpsimd if quad == 1 else nc.scalar).dma_start(w_sc[32 * quad : 32 * quad + 4, :], w_sc[4 * quad : 4 * quad + 4, :])
-        w_ord = [order_words(0), order_words(1)]
-        w_raw.append(load_words(2))
         warm = psum.tile([P, CHUNK], F32, name="warm", tag="bank6")
-        for n in range(5):
+        for n in range(WARM_UPS):
             nc.tensor.matmul_mx(
                 out=warm[:],
                 lhsT=table[:, 0 : P // 2].bitcast(U8).bitcast(FP4X4),
                 lhsT_scale=table_sc[:].bitcast(U8)[:, 0:P],
                 rhs=table[:, 0:CHUNK].bitcast(FP8X4),
-                rhs_scale=picked_sc0[:, 2 * CHUNK : 3 * CHUNK],
+                rhs_scale=picked_b[:, 0:CHUNK],
                 start=True,
                 stop=True,
             )
-        picked_sc1a = keep.tile([P, CHUNK], U8, name="picked_sc1a", align_bytes=64)
-        gather_scales(1, picked_sc1a, (0,))
+
+        w_ord = {}
+        for g in range(LISTS):
+            for a in range(PASSES):
+                w_ord[g, a] = keep.tile([P, R // 4], I32, name=f"w_ord{g}_{a}", align_bytes=64)
+                nc.scalar.copy(
+                    w_ord[g, a][:].bitcast(U32).rearrange("p (t q x) -> p t q x", t=PACK, x=4),
+                    w_raw[g][:, a * R // 4 : (a + 1) * R // 4].bitcast(U32).rearrange("p (q t x) -> p t q x", t=PACK, x=4),
+                )
+        cols = placed("cols", [P, PASSES, COLS], F32, 20 * KB)
+        nc.scalar.copy(cols[:], turned[:, :, 0:COLS])
+
         picked_words = {}
-        picked0 = keep.tile([P, LISTS, CHUNK], U32, name="picked0", align_bytes=64)
-        for g in range(LISTS):
-            picked_words[0, g] = gather_words(0, g, picked0[:, g, :])
-        cols = stage.tile([P, COLS], F32, name="cols", offset=37 * R)
-        nc.vector.tensor_copy(cols[:], turned[:, 0:COLS])
-        w_ord.append(order_words(2))
-        bias = keep.tile([P, N // P], F32, name="bias")
-        with nc.allow_non_contiguous_dma(reason="one bias value a partition"):
-            nc.gpsimd.dma_start(bias[:], b.rearrange("(m p) -> p m", p=P))
 
-        planes.append(stage.tile([P, LISTS * CHUNK // 4], I32, name="plane1", offset=4 * R, align_bytes=64))
-        wd_raw = stage.tile([P, SLOTS, N], F32, name="wd_raw", offset=5 * R + CHUNK, align_bytes=64)
-        wd_rows = wd.rearrange("(q s i) n -> s q (i n)", s=SLOTS, i=RUN)
+        def gather_words(c, tag):
+            picked = keep.tile([P, LISTS, CHUNK], U32, name=f"words{c}", tag=tag, align_bytes=64)
+            for g in range(LISTS):
+                nc.vector.tensor_copy(picked[:, g, :], table[:].bitcast(U32).indirect(list_slice(c, g)))
+                picked_words[c, g] = picked[:, g, :]
+
+        gather_words(0, "words0")
+        wd_raw = placed("wd_raw", [P, SLOTS, N], F32, 25 * KB)
+        wd_rows = wd.rearrange("(a q t i) n -> a t q (i n)", a=PASSES, t=PACK, i=RUN)
         for s in range(SLOTS):
-            nc.sync.dma_start(wd_raw[:, s, :], wd_rows[s])
-        move_scales(1, picked_sc1a, (0,))
-
-        picked_sc1b = stage.tile([P, 2 * CHUNK], U8, name="picked_sc1b", offset=36 * R, align_bytes=64)
-        gather_scales(1, picked_sc1b, (1, 2))
-        move_scales(1, picked_sc1b, (1, 2))
-        picked1 = keep.tile([P, LISTS, CHUNK], U32, name="picked1", tag="table_sc", align_bytes=64)
-        for g in range(LISTS):
-            picked_words[1, g] = gather_words(1, g, picked1[:, g, :])
+            nc.sync.dma_start(wd_raw[:, s, :], wd_rows[s // PACK][s % PACK])
+        bias = placed("bias", [P, N // P], F32, 24 * KB)
+        with nc.allow_non_contiguous_dma(reason="one bias value a partition"):
+            nc.sync.dma_start(bias[:], b.rearrange("(m p) -> p m", p=P))
+        scale_batch("c", ((1, 1), (1, 2)), 22 * KB, 35 * KB, nc.sync)
+        gather_words(1, "table_sc")
 
         def bank_of(c, s):
             return f"bank{(c * SLOTS + s) % BANKS}"
@@ -167,20 +160,16 @@ def tile_list_rvq_gelu_gelu_kernel(
         all_acts = []
 
         def weave_on_gpsimd(dst, values):
-            nc.gpsimd.tensor_scalar(dst.rearrange("p z t e -> p z e t"), values.rearrange("p z t e -> p z e t"), 1.0, 0.0, MULT, ADD)
+            nc.gpsimd.tensor_scalar(
+                dst.rearrange("p z t e -> p z e t"), values.rearrange("p z t e -> p z e t"), 1.0, 0.0, MULT, ADD
+            )
 
-        def scale_in_pairs(c, a, j_first, width, weaver):
-            scaled = keep.tile([P, PACK, width], BF16, name=f"scaled{c}_{a}", tag=f"scaled{c}_{a}", align_bytes=64)
-            woven = keep.tile([P, width, PACK], BF16, name=f"woven{c}_{a}", tag=f"woven{c}_{a}", align_bytes=64)
+        def scale_on_gpsimd(c, a, j_first, width, weaver):
+            scaled = keep.tile([P, PACK, width], BF16, name=f"scaled{c}_{a}", align_bytes=64)
+            woven = keep.tile([P, width, PACK], BF16, name=f"woven{c}_{a}", align_bytes=64)
             for t in range(PACK):
-                s = a * PACK + t
                 nc.gpsimd.tensor_scalar(
-                    scaled[:, t, :],
-                    all_acts[c][a][:, t, j_first : j_first + width],
-                    cols[:, s : s + 1],
-                    0.0,
-                    MULT,
-                    ADD,
+                    scaled[:, t, :], all_acts[c][a][:, t, j_first : j_first + width], cols[:, a, t : t + 1], 0.0, MULT, ADD
                 )
             for j0 in range(0, width, PIECE):
                 weaver[j0 // PIECE](
@@ -189,12 +178,8 @@ def tile_list_rvq_gelu_gelu_kernel(
                 )
             return woven
 
-        def scale_on_vector(c, a, j_first, width, parts=1):
-            if c == 0:
-                woven = stage.tile([P, width, PACK], BF16, name="h0_0", offset=20 * R, align_bytes=64)
-            else:
-                woven = keep.tile([P, width, PACK], BF16, name=f"h1_{a}_{j_first}", tag=("act0_0", "act1_0", "act0_1")[a + j_first // P], align_bytes=64)
-            factor = turned[:, a * PACK : (a + 1) * PACK].unsqueeze(1).unsqueeze(3)
+        def scale_on_vector(c, a, j_first, width, woven, parts=1):
+            factor = turned[:, a, 0:PACK].unsqueeze(1).unsqueeze(3)
             step = width // parts
             for j0 in range(0, width, step):
                 nc.vector.tensor_tensor(
@@ -205,69 +190,74 @@ def tile_list_rvq_gelu_gelu_kernel(
                 )
             return woven
 
-        def quantise(name, values, width, tag=None, parts=1, later=None):
-            if tag == "wd":
-                codes = stage.tile([P, width], U32, name="wd_codes", offset=24 * R, align_bytes=64)
-            else:
-                codes = keep.tile([P, width], U32, name=f"{name}_codes", tag=tag or f"{name}_codes", align_bytes=64)
+        def mx_tiles(name, width):
+            codes = keep.tile([P, width], U32, name=f"{name}_codes", align_bytes=64)
             plane = keep.tile([P, width], U8, name=f"{name}_sc", align_bytes=64)
-            step = width // parts
-
-            def part(j0):
-                nc.vector.quantize_mx(
-                    out=codes[:, j0 : j0 + step].bitcast(FP8X4),
-                    scales=plane[:, j0 : j0 + step],
-                    in_=values[:, PACK * j0 : PACK * (j0 + step)],
-                )
-
-            for j0 in range(0, width, step):
-                if later is not None and j0 > 0:
-                    later.append(lambda: part(step))
-                else:
-                    part(j0)
             return codes, plane
 
-        woven0 = []
-        for c in range(chunks):
-            acts = [keep.tile([P, PACK, CHUNK], F32, name=f"act{c}_{a}", tag=f"act{c}_{a}", align_bytes=64) for a in range(PASSES)]
+        def quantise(tiles, values, j0, width):
+            nc.vector.quantize_mx(
+                out=tiles[0][:, j0 : j0 + width].bitcast(FP8X4),
+                scales=tiles[1][:, j0 : j0 + width],
+                in_=values[:, j0 : j0 + width, :].rearrange("p j t -> p (j t)"),
+            )
+
+        def first_layer(c):
+            acts = [
+                keep.tile([P, PACK, CHUNK], F32, name=f"act{c}_{a}", tag=f"act{c}_{a}", align_bytes=64)
+                for a in range(PASSES)
+            ]
             all_acts.append(acts)
             accs = {}
             steps = [(s, g) for g in range(LISTS) for s in range(AHEAD[c])]
             steps.extend([(s, g) for s in range(AHEAD[c], SLOTS) for g in range(LISTS)])
             for s, g in steps:
+                a, t = divmod(s, PACK)
                 if g == 0:
                     accs[s] = psum.tile([P, CHUNK], F32, name=f"acc{c}_{s}", tag=bank_of(c, s))
                 nc.tensor.matmul_mx(
                     out=accs[s][:],
-                    lhsT=w_ord[g][:].bitcast(U8)[:, 2 * P * s : 2 * P * (s + 1)].bitcast(FP4X4),
+                    lhsT=w_ord[g, a][:].bitcast(U8)[:, 2 * P * t : 2 * P * (t + 1)].bitcast(FP4X4),
                     lhsT_scale=w_sc[:].bitcast(U8)[:, g * R + P * s : g * R + P * (s + 1)],
                     rhs=picked_words[c, g].bitcast(FP8X4),
-                    rhs_scale=planes[c][:].bitcast(U8)[:, g * CHUNK : (g + 1) * CHUNK],
+                    rhs_scale=plane_of[c, g],
                     start=(g == 0),
                     stop=(g == LISTS - 1),
                 )
                 if g == LISTS - 1:
                     step = PIECE if (c, s) == (chunks - 1, SLOTS - 1) else CHUNK
                     for j0 in range(0, CHUNK, step):
-                        nc.scalar.activation(acts[s // PACK][:, s % PACK, j0 : j0 + step], accs[s][:, j0 : j0 + step], GELU)
-            if c == 0:
-                wd_bf = stage.tile([P, PASSES, N, PACK], BF16, name="wd_bf", offset=16 * R, align_bytes=64)
-                for a in range(PASSES):
-                    wd_pass = wd_raw[:, a * PACK : (a + 1) * PACK, :].rearrange("p t n -> p n t")
-                    nc.gpsimd.tensor_scalar(wd_bf[:, a], wd_pass, 1.0, 0.0, MULT, ADD)
-                flat = "p j t -> p (j t)"
-                woven0.append(scale_on_vector(0, 0, 0, CHUNK))
-                wd_codes, wd_sc = quantise("wd", wd_bf[:].rearrange("p a n t -> p (a n t)"), PASSES * N, "wd")
-                woven0.append(scale_in_pairs(0, 1, 0, CHUNK, [weave_on_gpsimd, nc.scalar.copy]))
+                        nc.scalar.activation(acts[a][:, t, j0 : j0 + step], accs[s][:, j0 : j0 + step], GELU)
 
-        later = []
-        h0 = [quantise(f"h0_{a}", woven0[a][:].rearrange(flat), CHUNK, None, 1 + a, later) for a in range(PASSES)]
-        woven10 = [scale_on_vector(1, 0, half * PIECE, PIECE) for half in range(2)]
-        later[0]()
-        h10 = [quantise(f"h1_0{half}", woven10[half][:].rearrange(flat), PIECE) for half in range(2)]
-        h11 = [quantise("h1_1a", scale_on_vector(1, 1, 0, PIECE, 2)[:].rearrange(flat), PIECE, None, 2)]
-        last_woven = scale_in_pairs(1, 1, PIECE, PIECE, [nc.scalar.copy])
-        h11.append(quantise("h1_1b", last_woven[:].rearrange(flat), PIECE))
+        def shared(name, width, tag):
+            return keep.tile([P, width, PACK], BF16, name=name, tag=tag, align_bytes=64)
+
+        first_layer(0)
+        wd_bf = placed("wd_bf", [P, PASSES * N, PACK], BF16, 36 * KB)
+        for a in range(PASSES):
+            wd_pass = wd_raw[:, a * PACK : (a + 1) * PACK, :].rearrange("p t n -> p n t")
+            nc.gpsimd.tensor_scalar(wd_bf[:, a * N : (a + 1) * N, :], wd_pass, 1.0, 0.0, MULT, ADD)
+        woven00 = scale_on_vector(0, 0, 0, CHUNK, placed("h0_0", [P, CHUNK, PACK], BF16, 0))
+        wd_mx = (placed("wd_codes", [P, PASSES * N], U32, 4 * KB), keep.tile([P, PASSES * N], U8, name="wd_sc", align_bytes=64))
+        quantise(wd_mx, wd_bf, 0, PASSES * N)
+        woven01 = scale_on_gpsimd(0, 1, 0, CHUNK, [weave_on_gpsimd, nc.scalar.copy])
+        first_layer(1)
+
+        h0 = [mx_tiles(f"h0_{a}", CHUNK) for a in range(PASSES)]
+        quantise(h0[0], woven00, 0, CHUNK)
+        quantise(h0[1], woven01, 0, PIECE)
+        woven10 = [
+            scale_on_vector(1, 0, half * PIECE, PIECE, shared(f"h1_0{half}", PIECE, f"act0_{half}")) for half in range(2)
+        ]
+        quantise(h0[1], woven01, PIECE, PIECE)
+        h10 = [mx_tiles(f"h1_0{half}", PIECE) for half in range(2)]
+        for half in range(2):
+            quantise(h10[half], woven10[half], 0, PIECE)
+        h11 = [mx_tiles(f"h1_1{half}", PIECE) for half in range(2)]
+        woven11 = scale_on_vector(1, 1, 0, PIECE, shared("h1_10", PIECE, "act1_0"), 2)
+        for part in range(2):
+            quantise(h11[0], woven11, part * P, P)
+        quantise(h11[1], scale_on_gpsimd(1, 1, PIECE, PIECE, [nc.scalar.copy]), 0, PIECE)
 
         def open_banks(j0, width, follows):
             return [psum.tile([P, width], F32, name=f"y{j0}_{m}", tag=bank_of(1, follows[m])) for m in range(N // P)]
@@ -278,23 +268,21 @@ def tile_list_rvq_gelu_gelu_kernel(
                     first = a * N + m * P
                     nc.tensor.matmul_mx(
                         out=ybanks[m][:],
-                        lhsT=wd_codes[:, first : first + P].bitcast(FP8X4),
-                        lhsT_scale=wd_sc[:, first : first + P],
-                        rhs=operands[a][0].bitcast(FP8X4),
-                        rhs_scale=operands[a][1],
+                        lhsT=wd_mx[0][:, first : first + P].bitcast(FP8X4),
+                        lhsT_scale=wd_mx[1][:, first : first + P],
+                        rhs=operands[a][0][:].bitcast(FP8X4),
+                        rhs_scale=operands[a][1][:],
                         start=(a == 0),
                         stop=(a == PASSES - 1),
                     )
             for m in range(N // P if PASSES - 1 in passes else 0):
-                tag = f"result{j0}_{m}"
-                result = keep.tile([P, width], F32, name=f"result{j0}_{m}", tag=tag, align_bytes=64)
+                result = keep.tile([P, width], F32, name=f"result{j0}_{m}", align_bytes=64)
                 nc.scalar.activation(result[:], ybanks[m][:], GELU, bias=bias[:, m : m + 1])
                 nc.sync.dma_start(out[m * P : (m + 1) * P, j0 : j0 + width], result[:])
 
-        second_layer(0, CHUNK, [(codes[:], plane[:]) for codes, plane in h0], open_banks(0, CHUNK, (5, 6)), (0, 1))
+        second_layer(0, CHUNK, h0, open_banks(0, CHUNK, (5, 6)), (0, 1))
         halves = range(CHUNK // PIECE)
         last_banks = [open_banks(CHUNK + half * PIECE, PIECE, (1 + 2 * half, 2 + 2 * half)) for half in halves]
         for a in range(PASSES):
             for half in halves:
-                operands = [(h10[half][0][:], h10[half][1][:]), (h11[half][0][:], h11[half][1][:])]
-                second_layer(CHUNK + half * PIECE, PIECE, operands, last_banks[half], (a,))
+                second_layer(CHUNK + half * PIECE, PIECE, [h10[half], h11[half]], last_banks[half], (a,))

@@ -27,10 +27,10 @@ SCALE_ROWS = 16
 GROUP = 16
 PASSES = R // (P * PACK)
 SLOTS = PASSES * PACK
-BANKS = 7
+BANKS = 5
 CHUNK = 512
 PIECE = 256
-AHEAD = (4, 4)
+AHEAD = (4, 2)
 WARM_UPS = 5
 COLS = 8
 KB = 1024
@@ -57,19 +57,18 @@ def tile_list_rvq_gelu_gelu_kernel(
         table_sc = keep.tile([P, T // 4], I32, name="table_sc", tag="table_sc", align_bytes=64)
         nc.sync.dma_start(offsets[:], offs)
         nc.sync.dma_start(table_sc[P - SCALE_ROWS : P, :], tab_scales[0].bitcast(I32))
-        seed = placed("seed", [P, P], F32, 40 * KB)
+        seed = placed("seed", [P, P], F32, 19 * KB)
         nc.vector.memset(seed[:], 0.0)
         nc.vector.memset(table_sc[0 : P - SCALE_ROWS, :], 0)
-        sc_raw = placed("sc_raw", [SCALE_ROWS, LISTS * R // 4], I32, 16 * KB)
+        sc_raw = placed("sc_raw", [SCALE_ROWS, LISTS * R // 4], I32, 50 * KB)
         for g in range(LISTS):
             nc.sync.dma_start(sc_raw[:, g * R // 4 : (g + 1) * R // 4], w_scales[g][0].bitcast(I32))
         table_rows = tab_words[0].rearrange("p t i -> p (t i)").bitcast(I32)
         for half in range(2):
             columns = slice(half * T // 2, (half + 1) * T // 2)
             nc.sync.dma_start(table[:, columns], table_rows[:, columns])
-        w_raw = [placed(f"w_raw{g}", [P, R // 2], I32, (20, 24, 22)[g] * KB) for g in range(LISTS)]
-        for g in range(LISTS):
-            nc.sync.dma_start(w_raw[g][:], w_words[g][0].bitcast(I32))
+        w_raw = [placed(f"w_raw{g}", [P, R // 2], I32, (40 * KB, 48 * KB + 512, 52 * KB + 512)[g]) for g in range(LISTS)]
+        nc.sync.dma_start(w_raw[0][:], w_words[0][0].bitcast(I32))
 
         ident = keep.tile([P, P], F32, name="ident")
         make_identity(nc, ident[:])
@@ -82,13 +81,13 @@ def tile_list_rvq_gelu_gelu_kernel(
         for a in range(PASSES):
             nc.tensor.transpose(turned[:, a, :], rows[:, a, :], ident[:])
 
-        w_sc = placed("w_sc", [P, LISTS * R // 4], I32, 40 * KB)
+        w_sc = placed("w_sc", [P, LISTS * R // 4], I32, 19 * KB)
         nc.scalar.copy(
             w_sc[0:SCALE_ROWS, :].bitcast(U32).rearrange("p (z t q x) -> p z t q x", t=PACK, q=SCALE_ROWS, x=2),
             sc_raw[:].bitcast(U32).rearrange("p (z q t x) -> p z t q x", t=PACK, q=SCALE_ROWS, x=2),
         )
         for quad in range(1, QUADS):
-            nc.gpsimd.dma_start(w_sc[32 * quad : 32 * quad + 4, :], w_sc[4 * quad : 4 * quad + 4, :])
+            nc.scalar.dma_start(w_sc[32 * quad : 32 * quad + 4, :], w_sc[4 * quad : 4 * quad + 4, :])
 
         def list_slice(c, g):
             column = (g * J + c * CHUNK) // GROUP
@@ -109,8 +108,10 @@ def tile_list_rvq_gelu_gelu_kernel(
                 queue.dma_start(plane[32 * quad : 32 * quad + 4, :], picked[:].bitcast(I32)[first : first + 4, :])
             return picked
 
-        scale_batch("a", ((0, 0), (0, 1)), 19 * KB, 16 * KB, nc.scalar)
-        picked_b = scale_batch("b", ((0, 2), (1, 0)), 34 * KB, 19 * KB, nc.sync)
+        scale_batch("a", ((0, 0), (0, 1)), 22 * KB, 51 * KB, nc.scalar)
+        for g in range(1, LISTS):
+            nc.scalar.dma_start(w_raw[g][:], w_words[g][0].bitcast(I32))
+        picked_b = scale_batch("b", ((0, 2), (1, 0)), 24 * KB, 40 * KB + 256, nc.sync)
 
         warm = psum.tile([P, CHUNK], F32, name="warm", tag="bank6")
         for n in range(WARM_UPS):
@@ -132,7 +133,7 @@ def tile_list_rvq_gelu_gelu_kernel(
                     w_ord[g, a][:].bitcast(U32).rearrange("p (t q x) -> p t q x", t=PACK, x=4),
                     w_raw[g][:, a * R // 4 : (a + 1) * R // 4].bitcast(U32).rearrange("p (q t x) -> p t q x", t=PACK, x=4),
                 )
-        cols = placed("cols", [P, PASSES, COLS], F32, 20 * KB)
+        cols = placed("cols", [P, PASSES, COLS], F32, 40 * KB + 128)
         nc.scalar.copy(cols[:], turned[:, :, 0:COLS])
 
         picked_words = {}
@@ -144,14 +145,14 @@ def tile_list_rvq_gelu_gelu_kernel(
                 picked_words[c, g] = picked[:, g, :]
 
         gather_words(0, "words0")
-        wd_raw = placed("wd_raw", [P, SLOTS, N], F32, 25 * KB)
+        wd_raw = placed("wd_raw", [P, SLOTS, N], F32, 32 * KB + 64)
         wd_rows = wd.rearrange("(a q t i) n -> a t q (i n)", a=PASSES, t=PACK, i=RUN)
         for s in range(SLOTS):
             nc.sync.dma_start(wd_raw[:, s, :], wd_rows[s // PACK][s % PACK])
-        bias = placed("bias", [P, N // P], F32, 24 * KB)
+        bias = placed("bias", [P, N // P], F32, 40 * KB + 64)
         with nc.allow_non_contiguous_dma(reason="one bias value a partition"):
             nc.sync.dma_start(bias[:], b.rearrange("(m p) -> p m", p=P))
-        scale_batch("c", ((1, 1), (1, 2)), 22 * KB, 35 * KB, nc.sync)
+        scale_batch("c", ((1, 1), (1, 2)), 41 * KB + 256, 25 * KB, nc.sync)
         gather_words(1, "table_sc")
 
         def bank_of(c, s):
@@ -233,23 +234,25 @@ def tile_list_rvq_gelu_gelu_kernel(
             return keep.tile([P, width, PACK], BF16, name=name, tag=tag, align_bytes=64)
 
         first_layer(0)
-        wd_bf = placed("wd_bf", [P, PASSES * N, PACK], BF16, 36 * KB)
+        woven00 = scale_on_gpsimd(0, 0, 0, CHUNK, [weave_on_gpsimd, nc.scalar.copy])
+        wd_bf = placed("wd_bf", [P, PASSES * N, PACK], BF16, 26 * KB)
         for a in range(PASSES):
             wd_pass = wd_raw[:, a * PACK : (a + 1) * PACK, :].rearrange("p t n -> p n t")
             nc.gpsimd.tensor_scalar(wd_bf[:, a * N : (a + 1) * N, :], wd_pass, 1.0, 0.0, MULT, ADD)
-        woven00 = scale_on_vector(0, 0, 0, CHUNK, placed("h0_0", [P, CHUNK, PACK], BF16, 0))
+        woven01 = scale_on_vector(0, 1, 0, CHUNK, placed("h0_1", [P, CHUNK, PACK], BF16, 0))
         wd_mx = (placed("wd_codes", [P, PASSES * N], U32, 4 * KB), keep.tile([P, PASSES * N], U8, name="wd_sc", align_bytes=64))
-        quantise(wd_mx, wd_bf, 0, PASSES * N)
-        woven01 = scale_on_gpsimd(0, 1, 0, CHUNK, [weave_on_gpsimd, nc.scalar.copy])
         first_layer(1)
 
-        h0 = [mx_tiles(f"h0_{a}", CHUNK) for a in range(PASSES)]
+        h0 = [
+            (placed(f"h0_{a}_codes", [P, CHUNK], U32, (6 + 2 * a) * KB), keep.tile([P, CHUNK], U8, name=f"h0_{a}_sc", align_bytes=64))
+            for a in range(PASSES)
+        ]
         quantise(h0[0], woven00, 0, CHUNK)
-        quantise(h0[1], woven01, 0, PIECE)
+        quantise(wd_mx, wd_bf, 0, PASSES * N)
+        quantise(h0[1], woven01, 0, CHUNK)
         woven10 = [
             scale_on_vector(1, 0, half * PIECE, PIECE, shared(f"h1_0{half}", PIECE, f"act0_{half}")) for half in range(2)
         ]
-        quantise(h0[1], woven01, PIECE, PIECE)
         h10 = [mx_tiles(f"h1_0{half}", PIECE) for half in range(2)]
         for half in range(2):
             quantise(h10[half], woven10[half], 0, PIECE)
@@ -260,7 +263,7 @@ def tile_list_rvq_gelu_gelu_kernel(
         quantise(h11[1], scale_on_gpsimd(1, 1, PIECE, PIECE, [nc.scalar.copy]), 0, PIECE)
 
         def open_banks(j0, width, follows):
-            return [psum.tile([P, width], F32, name=f"y{j0}_{m}", tag=bank_of(1, follows[m])) for m in range(N // P)]
+            return [psum.tile([P, width], F32, name=f"y{j0}_{m}", tag=follows[m]) for m in range(N // P)]
 
         def second_layer(j0, width, operands, ybanks, passes):
             for a in passes:
@@ -280,9 +283,12 @@ def tile_list_rvq_gelu_gelu_kernel(
                 nc.scalar.activation(result[:], ybanks[m][:], GELU, bias=bias[:, m : m + 1])
                 nc.sync.dma_start(out[m * P : (m + 1) * P, j0 : j0 + width], result[:])
 
-        second_layer(0, CHUNK, h0, open_banks(0, CHUNK, (5, 6)), (0, 1))
+        second_layer(0, CHUNK, h0, open_banks(0, CHUNK, (bank_of(1, 3), bank_of(1, 4))), (0, 1))
         halves = range(CHUNK // PIECE)
-        last_banks = [open_banks(CHUNK + half * PIECE, PIECE, (1 + 2 * half, 2 + 2 * half)) for half in halves]
+        last_banks = [
+            open_banks(CHUNK, PIECE, ("bank5", "bank6")),
+            open_banks(CHUNK + PIECE, PIECE, (bank_of(1, 5), bank_of(1, 6))),
+        ]
         for a in range(PASSES):
             for half in halves:
                 second_layer(CHUNK + half * PIECE, PIECE, [h10[half], h11[half]], last_banks[half], (a,))

@@ -34,6 +34,10 @@ AHEAD = (4, 2)
 WARM_UPS = 5
 COLS = 8
 KB = 1024
+HALF = P // 2
+ACT_AT = 56 * KB
+WORDS_AT = 88 * KB
+SCALED_AT = 96 * KB
 
 
 def tile_list_rvq_gelu_gelu_kernel(
@@ -57,8 +61,6 @@ def tile_list_rvq_gelu_gelu_kernel(
         table_sc = keep.tile([P, T // 4], I32, name="table_sc", tag="table_sc", align_bytes=64)
         nc.sync.dma_start(offsets[:], offs)
         nc.sync.dma_start(table_sc[P - SCALE_ROWS : P, :], tab_scales[0].bitcast(I32))
-        seed = placed("seed", [P, P], F32, 19 * KB)
-        nc.vector.memset(seed[:], 0.0)
         nc.vector.memset(table_sc[0 : P - SCALE_ROWS, :], 0)
         sc_raw = placed("sc_raw", [SCALE_ROWS, LISTS * R // 4], I32, 50 * KB)
         for g in range(LISTS):
@@ -73,10 +75,13 @@ def tile_list_rvq_gelu_gelu_kernel(
         ident = keep.tile([P, P], F32, name="ident")
         make_identity(nc, ident[:])
         rows = keep.tile([P, PASSES, P], F32, name="rows", align_bytes=64)
-        nc.scalar.activation(rows[:], seed[:].unsqueeze(1).to_broadcast([P, PASSES, P]), GELU)
+        seed = placed("seed", [P, P], F32, 19 * KB)
+        nc.gpsimd.memset(seed[HALF:P], 0.0)
+        nc.gpsimd.memset(rows[0:HALF], 0.0)
         nc.gpsimd.dma_start(
             rows[0:PACK].rearrange("t a (q i) -> t (a q) i", i=RUN), sm.rearrange("(z t i) -> t z i", t=PACK, i=RUN)
         )
+        nc.scalar.activation(rows[HALF:P], seed[HALF:P].unsqueeze(1).to_broadcast([HALF, PASSES, P]), GELU)
         turned = psum.tile([P, PASSES, P], F32, name="turned", tag="vectors")
         for a in range(PASSES):
             nc.tensor.transpose(turned[:, a, :], rows[:, a, :], ident[:])
@@ -138,13 +143,12 @@ def tile_list_rvq_gelu_gelu_kernel(
 
         picked_words = {}
 
-        def gather_words(c, tag):
-            picked = keep.tile([P, LISTS, CHUNK], U32, name=f"words{c}", tag=tag, align_bytes=64)
+        def gather_words(c, picked):
             for g in range(LISTS):
                 nc.vector.tensor_copy(picked[:, g, :], table[:].bitcast(U32).indirect(list_slice(c, g)))
                 picked_words[c, g] = picked[:, g, :]
 
-        gather_words(0, "words0")
+        gather_words(0, placed("words0", [P, LISTS, CHUNK], U32, WORDS_AT))
         wd_raw = placed("wd_raw", [P, SLOTS, N], F32, 32 * KB + 64)
         wd_rows = wd.rearrange("(a q t i) n -> a t q (i n)", a=PASSES, t=PACK, i=RUN)
         for s in range(SLOTS):
@@ -153,7 +157,7 @@ def tile_list_rvq_gelu_gelu_kernel(
         with nc.allow_non_contiguous_dma(reason="one bias value a partition"):
             nc.sync.dma_start(bias[:], b.rearrange("(m p) -> p m", p=P))
         scale_batch("c", ((1, 1), (1, 2)), 41 * KB + 256, 25 * KB, nc.sync)
-        gather_words(1, "table_sc")
+        gather_words(1, keep.tile([P, LISTS, CHUNK], U32, name="words1", tag="table_sc", align_bytes=64))
 
         def bank_of(c, s):
             return f"bank{(c * SLOTS + s) % BANKS}"
@@ -165,17 +169,17 @@ def tile_list_rvq_gelu_gelu_kernel(
                 dst.rearrange("p z t e -> p z e t"), values.rearrange("p z t e -> p z e t"), 1.0, 0.0, MULT, ADD
             )
 
-        def scale_on_gpsimd(c, a, j_first, width, weaver):
-            scaled = keep.tile([P, PACK, width], BF16, name=f"scaled{c}_{a}", align_bytes=64)
-            woven = keep.tile([P, width, PACK], BF16, name=f"woven{c}_{a}", align_bytes=64)
+        def scale_on_gpsimd(c, a, j_first, width, weaver, woven):
+            scaled = placed(f"scaled{c}", [P, PACK, width], BF16, SCALED_AT + 4 * c * KB)
             for t in range(PACK):
                 nc.gpsimd.tensor_scalar(
                     scaled[:, t, :], all_acts[c][a][:, t, j_first : j_first + width], cols[:, a, t : t + 1], 0.0, MULT, ADD
                 )
-            for j0 in range(0, width, PIECE):
-                weaver[j0 // PIECE](
-                    woven[:, j0 : j0 + PIECE, :].rearrange("p (z e) t -> p z t e", e=4),
-                    scaled[:, :, j0 : j0 + PIECE].rearrange("p t (z e) -> p z t e", e=4),
+            step = width // 2
+            for half in range(2):
+                weaver[half](
+                    woven[half].rearrange("p (z e) t -> p z t e", e=4),
+                    scaled[:, :, half * step : (half + 1) * step].rearrange("p t (z e) -> p z t e", e=4),
                 )
             return woven
 
@@ -196,16 +200,17 @@ def tile_list_rvq_gelu_gelu_kernel(
             plane = keep.tile([P, width], U8, name=f"{name}_sc", align_bytes=64)
             return codes, plane
 
-        def quantise(tiles, values, j0, width):
+        def quantise(tiles, values, j0, width, source=None):
+            first = j0 if source is None else source
             nc.vector.quantize_mx(
                 out=tiles[0][:, j0 : j0 + width].bitcast(FP8X4),
                 scales=tiles[1][:, j0 : j0 + width],
-                in_=values[:, j0 : j0 + width, :].rearrange("p j t -> p (j t)"),
+                in_=values[:, first : first + width, :].rearrange("p j t -> p (j t)"),
             )
 
         def first_layer(c):
             acts = [
-                keep.tile([P, PACK, CHUNK], F32, name=f"act{c}_{a}", tag=f"act{c}_{a}", align_bytes=64)
+                placed(f"act{c}_{a}", [P, PACK, CHUNK], F32, ACT_AT + (2 * c + a) * 8 * KB)
                 for a in range(PASSES)
             ]
             all_acts.append(acts)
@@ -230,15 +235,24 @@ def tile_list_rvq_gelu_gelu_kernel(
                     for j0 in range(0, CHUNK, step):
                         nc.scalar.activation(acts[a][:, t, j0 : j0 + step], accs[s][:, j0 : j0 + step], GELU)
 
-        def shared(name, width, tag):
-            return keep.tile([P, width, PACK], BF16, name=name, tag=tag, align_bytes=64)
+        def shared(name, width, c, a):
+            return placed(name, [P, width, PACK], BF16, ACT_AT + (2 * c + a) * 8 * KB)
 
         first_layer(0)
-        woven00 = scale_on_gpsimd(0, 0, 0, CHUNK, [weave_on_gpsimd, nc.scalar.copy])
-        wd_bf = placed("wd_bf", [P, PASSES * N, PACK], BF16, 26 * KB)
-        for a in range(PASSES):
-            wd_pass = wd_raw[:, a * PACK : (a + 1) * PACK, :].rearrange("p t n -> p n t")
-            nc.gpsimd.tensor_scalar(wd_bf[:, a * N : (a + 1) * N, :], wd_pass, 1.0, 0.0, MULT, ADD)
+        wd_bf = [
+            placed("wd_bf0", [P, N, PACK], BF16, 10 * KB),
+            placed("wd_bf1", [P, N, PACK], BF16, ACT_AT + 2 * KB),
+        ]
+        woven00 = [
+            keep.tile([P, PIECE, PACK], BF16, name="h0_00", align_bytes=64),
+            placed("h0_01", [P, PIECE, PACK], BF16, WORDS_AT + 2 * KB),
+        ]
+        scale_on_gpsimd(0, 0, 0, CHUNK, [weave_on_gpsimd, nc.scalar.copy], [tile[:] for tile in woven00])
+        nc.gpsimd.tensor_scalar(wd_bf[1][:], wd_raw[:, PACK:SLOTS, :].rearrange("p t n -> p n t"), 1.0, 0.0, MULT, ADD)
+        nc.vector.tensor_copy(
+            wd_bf[0][:].rearrange("p (z e) t -> p z t e", e=4),
+            wd_raw[:, 0:PACK, :].rearrange("p t (z e) -> p z t e", e=4),
+        )
         woven01 = scale_on_vector(0, 1, 0, CHUNK, placed("h0_1", [P, CHUNK, PACK], BF16, 0))
         wd_mx = (placed("wd_codes", [P, PASSES * N], U32, 4 * KB), keep.tile([P, PASSES * N], U8, name="wd_sc", align_bytes=64))
         first_layer(1)
@@ -247,20 +261,24 @@ def tile_list_rvq_gelu_gelu_kernel(
             (placed(f"h0_{a}_codes", [P, CHUNK], U32, (6 + 2 * a) * KB), keep.tile([P, CHUNK], U8, name=f"h0_{a}_sc", align_bytes=64))
             for a in range(PASSES)
         ]
-        quantise(h0[0], woven00, 0, CHUNK)
-        quantise(wd_mx, wd_bf, 0, PASSES * N)
+        for half in range(2):
+            quantise(h0[0], woven00[half], half * PIECE, PIECE, 0)
+        quantise(wd_mx, wd_bf[0], 0, N, 0)
         quantise(h0[1], woven01, 0, CHUNK)
+        quantise(wd_mx, wd_bf[1], N, N, 0)
         woven10 = [
-            scale_on_vector(1, 0, half * PIECE, PIECE, shared(f"h1_0{half}", PIECE, f"act0_{half}")) for half in range(2)
+            scale_on_vector(1, 0, half * PIECE, PIECE, shared(f"h1_0{half}", PIECE, 0, half)) for half in range(2)
         ]
         h10 = [mx_tiles(f"h1_0{half}", PIECE) for half in range(2)]
         for half in range(2):
             quantise(h10[half], woven10[half], 0, PIECE)
         h11 = [mx_tiles(f"h1_1{half}", PIECE) for half in range(2)]
-        woven11 = scale_on_vector(1, 1, 0, PIECE, shared("h1_10", PIECE, "act1_0"), 2)
+        woven11 = scale_on_vector(1, 1, 0, PIECE, shared("h1_10", PIECE, 1, 0), 2)
         for part in range(2):
             quantise(h11[0], woven11, part * P, P)
-        quantise(h11[1], scale_on_gpsimd(1, 1, PIECE, PIECE, [nc.scalar.copy]), 0, PIECE)
+        last = keep.tile([P, PIECE, PACK], BF16, name="h1_11", align_bytes=64)
+        scale_on_gpsimd(1, 1, PIECE, PIECE, [weave_on_gpsimd, nc.scalar.copy], [last[:, 0:P, :], last[:, P:PIECE, :]])
+        quantise(h11[1], last, 0, PIECE)
 
         def open_banks(j0, width, follows):
             return [psum.tile([P, width], F32, name=f"y{j0}_{m}", tag=follows[m]) for m in range(N // P)]
@@ -279,7 +297,10 @@ def tile_list_rvq_gelu_gelu_kernel(
                         stop=(a == PASSES - 1),
                     )
             for m in range(N // P if PASSES - 1 in passes else 0):
-                result = keep.tile([P, width], F32, name=f"result{j0}_{m}", align_bytes=64)
+                if (j0, m) == (0, 1):
+                    result = placed("result_held", [P, width], F32, SCALED_AT + 4 * KB)
+                else:
+                    result = keep.tile([P, width], F32, name=f"result{j0}_{m}", align_bytes=64)
                 nc.scalar.activation(result[:], ybanks[m][:], GELU, bias=bias[:, m : m + 1])
                 nc.sync.dma_start(out[m * P : (m + 1) * P, j0 : j0 + width], result[:])
 

@@ -35,9 +35,7 @@ WARM_UPS = 5
 COLS = 8
 KB = 1024
 HALF = P // 2
-ACT_AT = 56 * KB
 WORDS_AT = 88 * KB
-SCALED_AT = 96 * KB
 
 
 def tile_list_rvq_gelu_gelu_kernel(
@@ -91,8 +89,6 @@ def tile_list_rvq_gelu_gelu_kernel(
             w_sc[0:SCALE_ROWS, :].bitcast(U32).rearrange("p (z t q x) -> p z t q x", t=PACK, q=SCALE_ROWS, x=2),
             sc_raw[:].bitcast(U32).rearrange("p (z q t x) -> p z t q x", t=PACK, q=SCALE_ROWS, x=2),
         )
-        for quad in range(1, QUADS):
-            nc.scalar.dma_start(w_sc[32 * quad : 32 * quad + 4, :], w_sc[4 * quad : 4 * quad + 4, :])
 
         def list_slice(c, g):
             column = (g * J + c * CHUNK) // GROUP
@@ -108,15 +104,21 @@ def tile_list_rvq_gelu_gelu_kernel(
                     picked[:, n * CHUNK : (n + 1) * CHUNK], table_sc[:].bitcast(U8).indirect(list_slice(c, g))
                 )
                 plane_of[c, g] = plane[:].bitcast(U8)[:, n * CHUNK : (n + 1) * CHUNK]
-            for quad in range(QUADS):
-                first = P - SCALE_ROWS + 4 * quad
-                queue.dma_start(plane[32 * quad : 32 * quad + 4, :], picked[:].bitcast(I32)[first : first + 4, :])
-            return picked
 
-        scale_batch("a", ((0, 0), (0, 1)), 22 * KB, 51 * KB, nc.scalar)
+            def move():
+                for quad in range(QUADS):
+                    first = P - SCALE_ROWS + 4 * quad
+                    queue.dma_start(plane[32 * quad : 32 * quad + 4, :], picked[:].bitcast(I32)[first : first + 4, :])
+
+            return picked, move
+
+        picked_a, move_a = scale_batch("a", ((0, 0), (0, 1), (0, 2)), 22 * KB, 50 * KB + 768, nc.scalar)
+        move_a()
+        for quad in range(1, QUADS):
+            nc.scalar.dma_start(w_sc[32 * quad : 32 * quad + 4, :], w_sc[4 * quad : 4 * quad + 4, :])
         for g in range(1, LISTS):
             nc.scalar.dma_start(w_raw[g][:], w_words[g][0].bitcast(I32))
-        picked_b = scale_batch("b", ((0, 2), (1, 0)), 24 * KB, 40 * KB + 256, nc.sync)
+        move_b = scale_batch("b", ((1, 0),), 24 * KB, 40 * KB + 256, nc.sync)[1]
 
         warm = psum.tile([P, CHUNK], F32, name="warm", tag="bank6")
         for n in range(WARM_UPS):
@@ -125,7 +127,7 @@ def tile_list_rvq_gelu_gelu_kernel(
                 lhsT=table[:, 0 : P // 2].bitcast(U8).bitcast(FP4X4),
                 lhsT_scale=table_sc[:].bitcast(U8)[:, 0:P],
                 rhs=table[:, 0:CHUNK].bitcast(FP8X4),
-                rhs_scale=picked_b[:, 0:CHUNK],
+                rhs_scale=picked_a[:, 2 * CHUNK : 3 * CHUNK],
                 start=True,
                 stop=True,
             )
@@ -156,7 +158,8 @@ def tile_list_rvq_gelu_gelu_kernel(
         bias = placed("bias", [P, N // P], F32, 40 * KB + 64)
         with nc.allow_non_contiguous_dma(reason="one bias value a partition"):
             nc.sync.dma_start(bias[:], b.rearrange("(m p) -> p m", p=P))
-        scale_batch("c", ((1, 1), (1, 2)), 41 * KB + 256, 25 * KB, nc.sync)
+        move_b()
+        scale_batch("c", ((1, 1), (1, 2)), 41 * KB + 256, 25 * KB, nc.sync)[1]()
         gather_words(1, keep.tile([P, LISTS, CHUNK], U32, name="words1", tag="table_sc", align_bytes=64))
 
         def bank_of(c, s):
@@ -169,17 +172,17 @@ def tile_list_rvq_gelu_gelu_kernel(
                 dst.rearrange("p z t e -> p z e t"), values.rearrange("p z t e -> p z e t"), 1.0, 0.0, MULT, ADD
             )
 
-        def scale_on_gpsimd(c, a, j_first, width, weaver, woven):
-            scaled = placed(f"scaled{c}", [P, PACK, width], BF16, SCALED_AT + 4 * c * KB)
+        def scale_on_gpsimd(c, a, j_first, width, weaver):
+            scaled = placed(f"scaled{c}", [P, PACK, width], BF16, (33 + 4 * c) * KB)
+            woven = keep.tile([P, width, PACK], BF16, name=f"woven{c}_{a}", align_bytes=64)
             for t in range(PACK):
                 nc.gpsimd.tensor_scalar(
                     scaled[:, t, :], all_acts[c][a][:, t, j_first : j_first + width], cols[:, a, t : t + 1], 0.0, MULT, ADD
                 )
-            step = width // 2
-            for half in range(2):
-                weaver[half](
-                    woven[half].rearrange("p (z e) t -> p z t e", e=4),
-                    scaled[:, :, half * step : (half + 1) * step].rearrange("p t (z e) -> p z t e", e=4),
+            for j0 in range(0, width, PIECE):
+                weaver[j0 // PIECE](
+                    woven[:, j0 : j0 + PIECE, :].rearrange("p (z e) t -> p z t e", e=4),
+                    scaled[:, :, j0 : j0 + PIECE].rearrange("p t (z e) -> p z t e", e=4),
                 )
             return woven
 
@@ -200,17 +203,16 @@ def tile_list_rvq_gelu_gelu_kernel(
             plane = keep.tile([P, width], U8, name=f"{name}_sc", align_bytes=64)
             return codes, plane
 
-        def quantise(tiles, values, j0, width, source=None):
-            first = j0 if source is None else source
+        def quantise(tiles, values, j0, width):
             nc.vector.quantize_mx(
                 out=tiles[0][:, j0 : j0 + width].bitcast(FP8X4),
                 scales=tiles[1][:, j0 : j0 + width],
-                in_=values[:, first : first + width, :].rearrange("p j t -> p (j t)"),
+                in_=values[:, j0 : j0 + width, :].rearrange("p j t -> p (j t)"),
             )
 
         def first_layer(c):
             acts = [
-                placed(f"act{c}_{a}", [P, PACK, CHUNK], F32, ACT_AT + (2 * c + a) * 8 * KB)
+                keep.tile([P, PACK, CHUNK], F32, name=f"act{c}_{a}", tag=f"act{c}_{a}", align_bytes=64)
                 for a in range(PASSES)
             ]
             all_acts.append(acts)
@@ -235,50 +237,35 @@ def tile_list_rvq_gelu_gelu_kernel(
                     for j0 in range(0, CHUNK, step):
                         nc.scalar.activation(acts[a][:, t, j0 : j0 + step], accs[s][:, j0 : j0 + step], GELU)
 
-        def shared(name, width, c, a):
-            return placed(name, [P, width, PACK], BF16, ACT_AT + (2 * c + a) * 8 * KB)
+        def shared(name, width, tag):
+            return keep.tile([P, width, PACK], BF16, name=name, tag=tag, align_bytes=64)
 
         first_layer(0)
-        wd_bf = [
-            placed("wd_bf0", [P, N, PACK], BF16, 10 * KB),
-            placed("wd_bf1", [P, N, PACK], BF16, ACT_AT + 2 * KB),
-        ]
-        woven00 = [
-            keep.tile([P, PIECE, PACK], BF16, name="h0_00", align_bytes=64),
-            placed("h0_01", [P, PIECE, PACK], BF16, WORDS_AT + 2 * KB),
-        ]
-        scale_on_gpsimd(0, 0, 0, CHUNK, [weave_on_gpsimd, nc.scalar.copy], [tile[:] for tile in woven00])
-        nc.gpsimd.tensor_scalar(wd_bf[1][:], wd_raw[:, PACK:SLOTS, :].rearrange("p t n -> p n t"), 1.0, 0.0, MULT, ADD)
-        nc.vector.tensor_copy(
-            wd_bf[0][:].rearrange("p (z e) t -> p z t e", e=4),
-            wd_raw[:, 0:PACK, :].rearrange("p t (z e) -> p z t e", e=4),
-        )
-        woven01 = scale_on_vector(0, 1, 0, CHUNK, placed("h0_1", [P, CHUNK, PACK], BF16, 0))
+        wd_bf = placed("wd_bf", [P, PASSES * N, PACK], BF16, 26 * KB)
+        for a in range(PASSES):
+            wd_pass = wd_raw[:, a * PACK : (a + 1) * PACK, :].rearrange("p t n -> p n t")
+            nc.gpsimd.tensor_scalar(wd_bf[:, a * N : (a + 1) * N, :], wd_pass, 1.0, 0.0, MULT, ADD)
+        woven00 = scale_on_vector(0, 0, 0, CHUNK, placed("h0_0", [P, CHUNK, PACK], BF16, 0))
         wd_mx = (placed("wd_codes", [P, PASSES * N], U32, 4 * KB), keep.tile([P, PASSES * N], U8, name="wd_sc", align_bytes=64))
+        quantise(wd_mx, wd_bf, 0, PASSES * N)
+        woven01 = scale_on_gpsimd(0, 1, 0, CHUNK, [weave_on_gpsimd, nc.scalar.copy])
         first_layer(1)
 
-        h0 = [
-            (placed(f"h0_{a}_codes", [P, CHUNK], U32, (6 + 2 * a) * KB), keep.tile([P, CHUNK], U8, name=f"h0_{a}_sc", align_bytes=64))
-            for a in range(PASSES)
-        ]
-        for half in range(2):
-            quantise(h0[0], woven00[half], half * PIECE, PIECE, 0)
-        quantise(wd_mx, wd_bf[0], 0, N, 0)
-        quantise(h0[1], woven01, 0, CHUNK)
-        quantise(wd_mx, wd_bf[1], N, N, 0)
+        h0 = [mx_tiles(f"h0_{a}", CHUNK) for a in range(PASSES)]
+        quantise(h0[0], woven00, 0, CHUNK)
+        quantise(h0[1], woven01, 0, PIECE)
         woven10 = [
-            scale_on_vector(1, 0, half * PIECE, PIECE, shared(f"h1_0{half}", PIECE, 0, half)) for half in range(2)
+            scale_on_vector(1, 0, half * PIECE, PIECE, shared(f"h1_0{half}", PIECE, f"act0_{half}")) for half in range(2)
         ]
+        quantise(h0[1], woven01, PIECE, PIECE)
         h10 = [mx_tiles(f"h1_0{half}", PIECE) for half in range(2)]
         for half in range(2):
             quantise(h10[half], woven10[half], 0, PIECE)
         h11 = [mx_tiles(f"h1_1{half}", PIECE) for half in range(2)]
-        woven11 = scale_on_vector(1, 1, 0, PIECE, shared("h1_10", PIECE, 1, 0), 2)
+        woven11 = scale_on_vector(1, 1, 0, PIECE, shared("h1_10", PIECE, "act1_0"), 2)
         for part in range(2):
             quantise(h11[0], woven11, part * P, P)
-        last = keep.tile([P, PIECE, PACK], BF16, name="h1_11", align_bytes=64)
-        scale_on_gpsimd(1, 1, PIECE, PIECE, [weave_on_gpsimd, nc.scalar.copy], [last[:, 0:P, :], last[:, P:PIECE, :]])
-        quantise(h11[1], last, 0, PIECE)
+        quantise(h11[1], scale_on_gpsimd(1, 1, PIECE, PIECE, [nc.scalar.copy]), 0, PIECE)
 
         def open_banks(j0, width, follows):
             return [psum.tile([P, width], F32, name=f"y{j0}_{m}", tag=follows[m]) for m in range(N // P)]
@@ -297,10 +284,7 @@ def tile_list_rvq_gelu_gelu_kernel(
                         stop=(a == PASSES - 1),
                     )
             for m in range(N // P if PASSES - 1 in passes else 0):
-                if (j0, m) == (0, 1):
-                    result = placed("result_held", [P, width], F32, SCALED_AT + 4 * KB)
-                else:
-                    result = keep.tile([P, width], F32, name=f"result{j0}_{m}", align_bytes=64)
+                result = keep.tile([P, width], F32, name=f"result{j0}_{m}", align_bytes=64)
                 nc.scalar.activation(result[:], ybanks[m][:], GELU, bias=bias[:, m : m + 1])
                 nc.sync.dma_start(out[m * P : (m + 1) * P, j0 : j0 + width], result[:])
 

@@ -36,6 +36,8 @@ COLS = 8
 KB = 1024
 HALF = P // 2
 WORDS_AT = 88 * KB
+WEAVE_AFTER = 2
+WEAVE_AT = 79 * KB
 
 
 def tile_list_rvq_gelu_gelu_kernel(
@@ -135,11 +137,13 @@ def tile_list_rvq_gelu_gelu_kernel(
         w_ord = {}
         for g in range(LISTS):
             for a in range(PASSES):
-                w_ord[g, a] = keep.tile([P, R // 4], I32, name=f"w_ord{g}_{a}", align_bytes=64)
-                nc.scalar.copy(
-                    w_ord[g, a][:].bitcast(U32).rearrange("p (t q x) -> p t q x", t=PACK, x=4),
-                    w_raw[g][:, a * R // 4 : (a + 1) * R // 4].bitcast(U32).rearrange("p (q t x) -> p t q x", t=PACK, x=4),
-                )
+                source = w_raw[g][:, a * R // 4 : (a + 1) * R // 4].bitcast(U32).rearrange("p (q t x) -> p t q x", t=PACK, x=4)
+                for t0, t1 in ((0, WEAVE_AFTER + 1), (WEAVE_AFTER + 1, PACK)) if (g, a) == (LISTS - 1, 0) else ((0, PACK),):
+                    at = WEAVE_AT if t1 < PACK else (70 + 2 * g + a) * KB
+                    ordered = placed(f"w_ord{g}_{a}_{t0}", [P, t1 - t0, P // 2], I32, at)
+                    nc.scalar.copy(ordered[:].bitcast(U32).rearrange("p t (q x) -> p t q x", x=4), source[:, t0:t1])
+                    for t in range(t0, t1):
+                        w_ord[g, a, t] = ordered[:, t - t0, :]
         cols = placed("cols", [P, PASSES, COLS], F32, 40 * KB + 128)
         nc.scalar.copy(cols[:], turned[:, :, 0:COLS])
 
@@ -172,18 +176,20 @@ def tile_list_rvq_gelu_gelu_kernel(
                 dst.rearrange("p z t e -> p z e t"), values.rearrange("p z t e -> p z e t"), 1.0, 0.0, MULT, ADD
             )
 
-        def scale_on_gpsimd(c, a, j_first, width, weaver):
+        def scale_on_gpsimd(c, a, j_first, width):
             scaled = placed(f"scaled{c}", [P, PACK, width], BF16, (33 + 4 * c) * KB)
-            woven = keep.tile([P, width, PACK], BF16, name=f"woven{c}_{a}", align_bytes=64)
             for t in range(PACK):
                 nc.gpsimd.tensor_scalar(
                     scaled[:, t, :], all_acts[c][a][:, t, j_first : j_first + width], cols[:, a, t : t + 1], 0.0, MULT, ADD
                 )
-            for j0 in range(0, width, PIECE):
-                weaver[j0 // PIECE](
-                    woven[:, j0 : j0 + PIECE, :].rearrange("p (z e) t -> p z t e", e=4),
-                    scaled[:, :, j0 : j0 + PIECE].rearrange("p t (z e) -> p z t e", e=4),
-                )
+            return scaled
+
+        def weave(weaver, scaled, j0, name, at):
+            woven = placed(name, [P, PIECE, PACK], BF16, at)
+            weaver(
+                woven[:].rearrange("p (z e) t -> p z t e", e=4),
+                scaled[:, :, j0 : j0 + PIECE].rearrange("p t (z e) -> p z t e", e=4),
+            )
             return woven
 
         def scale_on_vector(c, a, j_first, width, woven, parts=1):
@@ -203,14 +209,14 @@ def tile_list_rvq_gelu_gelu_kernel(
             plane = keep.tile([P, width], U8, name=f"{name}_sc", align_bytes=64)
             return codes, plane
 
-        def quantise(tiles, values, j0, width):
+        def quantise(tiles, values, j0, width, at=0):
             nc.vector.quantize_mx(
-                out=tiles[0][:, j0 : j0 + width].bitcast(FP8X4),
-                scales=tiles[1][:, j0 : j0 + width],
+                out=tiles[0][:, at + j0 : at + j0 + width].bitcast(FP8X4),
+                scales=tiles[1][:, at + j0 : at + j0 + width],
                 in_=values[:, j0 : j0 + width, :].rearrange("p j t -> p (j t)"),
             )
 
-        def first_layer(c):
+        def first_layer(c, between):
             acts = [
                 keep.tile([P, PACK, CHUNK], F32, name=f"act{c}_{a}", tag=f"act{c}_{a}", align_bytes=64)
                 for a in range(PASSES)
@@ -225,7 +231,7 @@ def tile_list_rvq_gelu_gelu_kernel(
                     accs[s] = psum.tile([P, CHUNK], F32, name=f"acc{c}_{s}", tag=bank_of(c, s))
                 nc.tensor.matmul_mx(
                     out=accs[s][:],
-                    lhsT=w_ord[g, a][:].bitcast(U8)[:, 2 * P * t : 2 * P * (t + 1)].bitcast(FP4X4),
+                    lhsT=w_ord[g, a, t].bitcast(U8).bitcast(FP4X4),
                     lhsT_scale=w_sc[:].bitcast(U8)[:, g * R + P * s : g * R + P * (s + 1)],
                     rhs=picked_words[c, g].bitcast(FP8X4),
                     rhs_scale=plane_of[c, g],
@@ -233,6 +239,8 @@ def tile_list_rvq_gelu_gelu_kernel(
                     stop=(g == LISTS - 1),
                 )
                 if g == LISTS - 1:
+                    if s == WEAVE_AFTER:
+                        between()
                     step = PIECE if (c, s) == (chunks - 1, SLOTS - 1) else CHUNK
                     for j0 in range(0, CHUNK, step):
                         nc.scalar.activation(acts[a][:, t, j0 : j0 + step], accs[s][:, j0 : j0 + step], GELU)
@@ -240,7 +248,7 @@ def tile_list_rvq_gelu_gelu_kernel(
         def shared(name, width, tag):
             return keep.tile([P, width, PACK], BF16, name=name, tag=tag, align_bytes=64)
 
-        first_layer(0)
+        first_layer(0, lambda: None)
         wd_bf = placed("wd_bf", [P, PASSES * N, PACK], BF16, 26 * KB)
         for a in range(PASSES):
             wd_pass = wd_raw[:, a * PACK : (a + 1) * PACK, :].rearrange("p t n -> p n t")
@@ -248,16 +256,17 @@ def tile_list_rvq_gelu_gelu_kernel(
         woven00 = scale_on_vector(0, 0, 0, CHUNK, placed("h0_0", [P, CHUNK, PACK], BF16, 0))
         wd_mx = (placed("wd_codes", [P, PASSES * N], U32, 4 * KB), keep.tile([P, PASSES * N], U8, name="wd_sc", align_bytes=64))
         quantise(wd_mx, wd_bf, 0, PASSES * N)
-        woven01 = scale_on_gpsimd(0, 1, 0, CHUNK, [weave_on_gpsimd, nc.scalar.copy])
-        first_layer(1)
+        scaled01 = scale_on_gpsimd(0, 1, 0, CHUNK)
+        woven01 = [weave(weave_on_gpsimd, scaled01, 0, "woven01a", 82 * KB)]
+        first_layer(1, lambda: woven01.append(weave(nc.scalar.copy, scaled01, PIECE, "woven01b", WEAVE_AT)))
 
         h0 = [mx_tiles(f"h0_{a}", CHUNK) for a in range(PASSES)]
         quantise(h0[0], woven00, 0, CHUNK)
-        quantise(h0[1], woven01, 0, PIECE)
+        quantise(h0[1], woven01[0], 0, PIECE)
         woven10 = [
             scale_on_vector(1, 0, half * PIECE, PIECE, shared(f"h1_0{half}", PIECE, f"act0_{half}")) for half in range(2)
         ]
-        quantise(h0[1], woven01, PIECE, PIECE)
+        quantise(h0[1], woven01[1], 0, PIECE, PIECE)
         h10 = [mx_tiles(f"h1_0{half}", PIECE) for half in range(2)]
         for half in range(2):
             quantise(h10[half], woven10[half], 0, PIECE)
@@ -265,7 +274,7 @@ def tile_list_rvq_gelu_gelu_kernel(
         woven11 = scale_on_vector(1, 1, 0, PIECE, shared("h1_10", PIECE, "act1_0"), 2)
         for part in range(2):
             quantise(h11[0], woven11, part * P, P)
-        quantise(h11[1], scale_on_gpsimd(1, 1, PIECE, PIECE, [nc.scalar.copy]), 0, PIECE)
+        quantise(h11[1], weave(nc.scalar.copy, scale_on_gpsimd(1, 1, PIECE, PIECE), 0, "woven11b", 96 * KB), 0, PIECE)
 
         def open_banks(j0, width, follows):
             return [psum.tile([P, width], F32, name=f"y{j0}_{m}", tag=follows[m]) for m in range(N // P)]

@@ -22,7 +22,6 @@ ADD = mybir.AluOpType.add
 P = 128
 PACK = 4
 RUN = 8
-QUADS = 4
 SCALE_ROWS = 16
 GROUP = 16
 PASSES = R // (P * PACK)
@@ -108,15 +107,14 @@ def tile_list_rvq_gelu_gelu_kernel(
                 plane_of[c, g] = plane[:].bitcast(U8)[:, n * CHUNK : (n + 1) * CHUNK]
 
             def move():
-                for quad in range(QUADS):
-                    first = P - SCALE_ROWS + 4 * quad
-                    queue.dma_start(plane[32 * quad : 32 * quad + 4, :], picked[:].bitcast(I32)[first : first + 4, :])
+                for x in range(4):
+                    queue.dma_start(plane[x:P:32, :], picked[:].bitcast(I32)[P - SCALE_ROWS + x : P : 4, :])
 
             return picked, move
 
         picked_a, move_a = scale_batch("a", ((0, 0), (0, 1), (0, 2)), 22 * KB, 50 * KB + 768, nc.scalar)
         move_a()
-        for quad in range(1, QUADS):
+        for quad in (2, 1, 3):
             nc.scalar.dma_start(w_sc[32 * quad : 32 * quad + 4, :], w_sc[4 * quad : 4 * quad + 4, :])
         for g in range(1, LISTS):
             nc.scalar.dma_start(w_raw[g][:], w_words[g][0].bitcast(I32))

from contextlib import ExitStack

import concourse.mybir as mybir
from concourse.masks import make_identity

K, R, N, T, J = 512, 1024, 256, 4096, 1024
LISTS = 3
FLOPS = 2 * LISTS * K * R * J + 2 * R * N * J

F32 = mybir.dt.float32
BF16 = mybir.dt.bfloat16
I32 = mybir.dt.int32
U32 = mybir.dt.uint32
U16 = mybir.dt.uint16
U8 = mybir.dt.uint8
FP8X4 = mybir.dt.float8_e4m3fn_x4
FP4X4 = mybir.dt.float4_e2m1fn_x4
GELU = mybir.ActivationFunctionType.Gelu_apprx_tanh
MULT = mybir.AluOpType.mult
ADD = mybir.AluOpType.add

P = 128
PACK = 4
RUN = 8
SCALE_ROWS = 16
GROUP = 16
PASSES = R // (P * PACK)
SLOTS = PASSES * PACK
BANKS = 5
CHUNK = 512
PIECE = 256
AHEAD = (4, 2)
WARM_UPS = 5
COLS = 8
KB = 1024
HALF = P // 2
WORDS_AT = 88 * KB
WEAVE_AFTER = 2
WEAVE_AT = 79 * KB


def tile_list_rvq_gelu_gelu_kernel(
    tc, tab_words, tab_scales, w0_words, w0_scales, w1_words, w1_scales, w2_words, w2_scales, sm, wd, b, offs, out
):
    nc = tc.nc
    w_words = (w0_words, w1_words, w2_words)
    w_scales = (w0_scales, w1_scales, w2_scales)
    chunks = J // CHUNK

    with ExitStack() as ctx:
        keep = ctx.enter_context(tc.tile_pool(name="keep", bufs=1))
        stage = ctx.enter_context(tc.tile_pool(name="stage", bufs=1))
        psum = ctx.enter_context(tc.psum_pool(name="psum", bufs=1))

        def placed(name, shape, dtype, offset):
            return stage.tile(shape, dtype, name=name, offset=offset, align_bytes=64)

        offsets = keep.tile([P, LISTS * J // GROUP], U16, name="offsets")
        table = placed("table", [P, T], I32, 0)
        table_sc = keep.tile([P, T // 4], I32, name="table_sc", tag="table_sc", align_bytes=64)
        nc.sync.dma_start(offsets[:], offs)
        nc.sync.dma_start(table_sc[P - SCALE_ROWS : P, :], tab_scales[0].bitcast(I32))
        nc.vector.memset(table_sc[0 : P - SCALE_ROWS, :], 0)
        sc_raw = placed("sc_raw", [SCALE_ROWS, LISTS * R // 4], I32, 50 * KB)
        for g in range(LISTS):
            nc.sync.dma_start(sc_raw[:, g * R // 4 : (g + 1) * R // 4], w_scales[g][0].bitcast(I32))
        table_rows = tab_words[0].rearrange("p t i -> p (t i)").bitcast(I32)
        for half in range(2):
            columns = slice(half * T // 2, (half + 1) * T // 2)
            nc.sync.dma_start(table[:, columns], table_rows[:, columns])
        w_raw = [placed(f"w_raw{g}", [P, R // 2], I32, (40 * KB, 48 * KB + 512, 52 * KB + 512)[g]) for g in range(LISTS)]
        nc.sync.dma_start(w_raw[0][:], w_words[0][0].bitcast(I32))

        ident = keep.tile([P, P], F32, name="ident")
        make_identity(nc, ident[:])
        rows = keep.tile([P, PASSES, P], F32, name="rows", align_bytes=64)
        seed = placed("seed", [P, P], F32, 19 * KB)
        nc.gpsimd.memset(seed[HALF:P], 0.0)
        nc.gpsimd.memset(rows[0:HALF], 0.0)
        nc.gpsimd.dma_start(
            rows[0:PACK].rearrange("t a (q i) -> t (a q) i", i=RUN), sm.rearrange("(z t i) -> t z i", t=PACK, i=RUN)
        )
        nc.scalar.activation(rows[HALF:P], seed[HALF:P].unsqueeze(1).to_broadcast([HALF, PASSES, P]), GELU)
        turned = psum.tile([P, PASSES, P], F32, name="turned", tag="vectors")
        for a in range(PASSES):
            nc.tensor.transpose(turned[:, a, :], rows[:, a, :], ident[:])

        w_sc = placed("w_sc", [P, LISTS * R // 4], I32, 19 * KB)
        nc.scalar.copy(
            w_sc[0:SCALE_ROWS, :].bitcast(U32).rearrange("p (z t q x) -> p z t q x", t=PACK, q=SCALE_ROWS, x=2),
            sc_raw[:].bitcast(U32).rearrange("p (z q t x) -> p z t q x", t=PACK, q=SCALE_ROWS, x=2),
        )

        def list_slice(c, g):
            column = (g * J + c * CHUNK) // GROUP
            return offsets[:, column : column + CHUNK // GROUP]

        plane_of = {}

        def scale_batch(name, members, picked_at, plane_at, queue):
            picked = placed(f"picked_{name}", [P, len(members) * CHUNK], U8, picked_at)
            plane = placed(f"plane_{name}", [P, len(members) * CHUNK // 4], I32, plane_at)
            for n, (c, g) in enumerate(members):
                nc.vector.tensor_copy(
                    picked[:, n * CHUNK : (n + 1) * CHUNK], table_sc[:].bitcast(U8).indirect(list_slice(c, g))
                )
                plane_of[c, g] = plane[:].bitcast(U8)[:, n * CHUNK : (n + 1) * CHUNK]

            def move():
                for x in range(4):
                    queue.dma_start(plane[x:P:32, :], picked[:].bitcast(I32)[P - SCALE_ROWS + x : P : 4, :])

            return picked, move

        picked_a, move_a = scale_batch("a", ((0, 0), (0, 1), (0, 2)), 22 * KB, 50 * KB + 768, nc.scalar)
        move_a()
        for quad in (2, 1, 3):
            nc.scalar.dma_start(w_sc[32 * quad : 32 * quad + 4, :], w_sc[4 * quad : 4 * quad + 4, :])
        for g in range(1, LISTS):
            nc.scalar.dma_start(w_raw[g][:], w_words[g][0].bitcast(I32))
        move_b = scale_batch("b", ((1, 0),), 24 * KB, 40 * KB + 256, nc.sync)[1]

        warm = psum.tile([P, CHUNK], F32, name="warm", tag="bank6")
        for n in range(WARM_UPS):
            nc.tensor.matmul_mx(
                out=warm[:],
                lhsT=table[:, 0 : P // 2].bitcast(U8).bitcast(FP4X4),
                lhsT_scale=table_sc[:].bitcast(U8)[:, 0:P],
                rhs=table[:, 0:CHUNK].bitcast(FP8X4),
                rhs_scale=picked_a[:, 2 * CHUNK : 3 * CHUNK],
                start=True,
                stop=True,
            )

        w_ord = {}
        for g in range(LISTS):
            for a in range(PASSES):
                source = w_raw[g][:, a * R // 4 : (a + 1) * R // 4].bitcast(U32).rearrange("p (q t x) -> p t q x", t=PACK, x=4)
                for t0, t1 in ((0, WEAVE_AFTER + 1), (WEAVE_AFTER + 1, PACK)) if (g, a) == (LISTS - 1, 0) else ((0, PACK),):
                    at = WEAVE_AT if t1 < PACK else (70 + 2 * g + a) * KB
                    ordered = placed(f"w_ord{g}_{a}_{t0}", [P, t1 - t0, P // 2], I32, at)
                    nc.scalar.copy(ordered[:].bitcast(U32).rearrange("p t (q x) -> p t q x", x=4), source[:, t0:t1])
                    for t in range(t0, t1):
                        w_ord[g, a, t] = ordered[:, t - t0, :]
        cols = placed("cols", [P, PASSES, COLS], F32, 40 * KB + 128)
        nc.scalar.copy(cols[:], turned[:, :, 0:COLS])

        picked_words = {}

        def gather_words(c, picked):
            for g in range(LISTS):
                nc.vector.tensor_copy(picked[:, g, :], table[:].bitcast(U32).indirect(list_slice(c, g)))
                picked_words[c, g] = picked[:, g, :]

        gather_words(0, placed("words0", [P, LISTS, CHUNK], U32, WORDS_AT))
        wd_raw = placed("wd_raw", [P, SLOTS, N], F32, 32 * KB + 64)
        wd_rows = wd.rearrange("(a q t i) n -> a t q (i n)", a=PASSES, t=PACK, i=RUN)
        for s in range(SLOTS):
            nc.sync.dma_start(wd_raw[:, s, :], wd_rows[s // PACK][s % PACK])
        bias = placed("bias", [P, N // P], F32, 40 * KB + 64)
        with nc.allow_non_contiguous_dma(reason="one bias value a partition"):
            nc.sync.dma_start(bias[:], b.rearrange("(m p) -> p m", p=P))
        move_b()
        scale_batch("c", ((1, 1), (1, 2)), 41 * KB + 256, 25 * KB, nc.sync)[1]()
        gather_words(1, keep.tile([P, LISTS, CHUNK], U32, name="words1", tag="table_sc", align_bytes=64))

        def bank_of(c, s):
            return f"bank{(c * SLOTS + s) % BANKS}"

        all_acts = []

        def weave_on_gpsimd(dst, values):
            nc.gpsimd.tensor_scalar(
                dst.rearrange("p z t e -> p z e t"), values.rearrange("p z t e -> p z e t"), 1.0, 0.0, MULT, ADD
            )

        def scale_on_gpsimd(c, a, j_first, width):
            scaled = placed(f"scaled{c}", [P, PACK, width], BF16, (33 + 4 * c) * KB)
            for t in range(PACK):
                nc.gpsimd.tensor_scalar(
                    scaled[:, t, :], all_acts[c][a][:, t, j_first : j_first + width], cols[:, a, t : t + 1], 0.0, MULT, ADD
                )
            return scaled

        def weave(weaver, scaled, j0, name, at):
            woven = placed(name, [P, PIECE, PACK], BF16, at)
            weaver(
                woven[:].rearrange("p (z e) t -> p z t e", e=4),
                scaled[:, :, j0 : j0 + PIECE].rearrange("p t (z e) -> p z t e", e=4),
            )
            return woven

        def scale_on_vector(c, a, j_first, width, woven, parts=1):
            factor = turned[:, a, 0:PACK].unsqueeze(1).unsqueeze(3)
            step = width // parts
            for j0 in range(0, width, step):
                nc.vector.tensor_tensor(
                    woven[:, j0 : j0 + step, :].rearrange("p (z e) t -> p z t e", e=2),
                    all_acts[c][a][:, :, j_first + j0 : j_first + j0 + step].rearrange("p t (z e) -> p z t e", e=2),
                    factor.to_broadcast([P, step // 2, PACK, 2]),
                    MULT,
                )
            return woven

        def mx_tiles(name, width):
            codes = keep.tile([P, width], U32, name=f"{name}_codes", align_bytes=64)
            plane = keep.tile([P, width], U8, name=f"{name}_sc", align_bytes=64)
            return codes, plane

        def quantise(tiles, values, j0, width, at=0):
            nc.vector.quantize_mx(
                out=tiles[0][:, at + j0 : at + j0 + width].bitcast(FP8X4),
                scales=tiles[1][:, at + j0 : at + j0 + width],
                in_=values[:, j0 : j0 + width, :].rearrange("p j t -> p (j t)"),
            )

        def first_layer(c, between):
            acts = [
                keep.tile([P, PACK, CHUNK], F32, name=f"act{c}_{a}", tag=f"act{c}_{a}", align_bytes=64)
                for a in range(PASSES)
            ]
            all_acts.append(acts)
            accs = {}
            steps = [(s, g) for g in range(LISTS) for s in range(AHEAD[c])]
            steps.extend([(s, g) for s in range(AHEAD[c], SLOTS) for g in range(LISTS)])
            for s, g in steps:
                a, t = divmod(s, PACK)
                if g == 0:
                    accs[s] = psum.tile([P, CHUNK], F32, name=f"acc{c}_{s}", tag=bank_of(c, s))
                nc.tensor.matmul_mx(
                    out=accs[s][:],
                    lhsT=w_ord[g, a, t].bitcast(U8).bitcast(FP4X4),
                    lhsT_scale=w_sc[:].bitcast(U8)[:, g * R + P * s : g * R + P * (s + 1)],
                    rhs=picked_words[c, g].bitcast(FP8X4),
                    rhs_scale=plane_of[c, g],
                    start=(g == 0),
                    stop=(g == LISTS - 1),
                )
                if g == LISTS - 1:
                    if s == WEAVE_AFTER:
                        between()
                    step = PIECE if (c, s) == (chunks - 1, SLOTS - 1) else CHUNK
                    for j0 in range(0, CHUNK, step):
                        nc.scalar.activation(acts[a][:, t, j0 : j0 + step], accs[s][:, j0 : j0 + step], GELU)

        def shared(name, width, tag):
            return keep.tile([P, width, PACK], BF16, name=name, tag=tag, align_bytes=64)

        first_layer(0, lambda: None)
        wd_bf = placed("wd_bf", [P, PASSES * N, PACK], BF16, 26 * KB)
        for a in range(PASSES):
            wd_pass = wd_raw[:, a * PACK : (a + 1) * PACK, :].rearrange("p t n -> p n t")
            nc.gpsimd.tensor_scalar(wd_bf[:, a * N : (a + 1) * N, :], wd_pass, 1.0, 0.0, MULT, ADD)
        woven00 = scale_on_vector(0, 0, 0, CHUNK, placed("h0_0", [P, CHUNK, PACK], BF16, 0))
        wd_mx = (placed("wd_codes", [P, PASSES * N], U32, 4 * KB), keep.tile([P, PASSES * N], U8, name="wd_sc", align_bytes=64))
        quantise(wd_mx, wd_bf, 0, PASSES * N)
        scaled01 = scale_on_gpsimd(0, 1, 0, CHUNK)
        woven01 = [weave(weave_on_gpsimd, scaled01, 0, "woven01a", 82 * KB)]
        first_layer(1, lambda: woven01.append(weave(nc.scalar.copy, scaled01, PIECE, "woven01b", WEAVE_AT)))

        h0 = [mx_tiles(f"h0_{a}", CHUNK) for a in range(PASSES)]
        quantise(h0[0], woven00, 0, CHUNK)
        quantise(h0[1], woven01[0], 0, PIECE)
        woven10 = [
            scale_on_vector(1, 0, half * PIECE, PIECE, shared(f"h1_0{half}", PIECE, f"act0_{half}")) for half in range(2)
        ]
        quantise(h0[1], woven01[1], 0, PIECE, PIECE)
        h10 = [mx_tiles(f"h1_0{half}", PIECE) for half in range(2)]
        for half in range(2):
            quantise(h10[half], woven10[half], 0, PIECE)
        h11 = [mx_tiles(f"h1_1{half}", PIECE) for half in range(2)]
        woven11 = scale_on_vector(1, 1, 0, PIECE, shared("h1_10", PIECE, "act1_0"), 2)
        for part in range(2):
            quantise(h11[0], woven11, part * P, P)
        quantise(h11[1], weave(nc.scalar.copy, scale_on_gpsimd(1, 1, PIECE, PIECE), 0, "woven11b", 96 * KB), 0, PIECE)

        def open_banks(j0, width, follows):
            return [psum.tile([P, width], F32, name=f"y{j0}_{m}", tag=follows[m]) for m in range(N // P)]

        def second_layer(j0, width, operands, ybanks, passes):
            for a in passes:
                for m in range(N // P):
                    first = a * N + m * P
                    nc.tensor.matmul_mx(
                        out=ybanks[m][:],
                        lhsT=wd_mx[0][:, first : first + P].bitcast(FP8X4),
                        lhsT_scale=wd_mx[1][:, first : first + P],
                        rhs=operands[a][0][:].bitcast(FP8X4),
                        rhs_scale=operands[a][1][:],
                        start=(a == 0),
                        stop=(a == PASSES - 1),
                    )
            for m in range(N // P if PASSES - 1 in passes else 0):
                result = keep.tile([P, width], F32, name=f"result{j0}_{m}", align_bytes=64)
                nc.scalar.activation(result[:], ybanks[m][:], GELU, bias=bias[:, m : m + 1])
                nc.sync.dma_start(out[m * P : (m + 1) * P, j0 : j0 + width], result[:])

        second_layer(0, CHUNK, h0, open_banks(0, CHUNK, (bank_of(1, 3), bank_of(1, 4))), (0, 1))
        halves = range(CHUNK // PIECE)
        last_banks = [
            open_banks(CHUNK, PIECE, ("bank5", "bank6")),
            open_banks(CHUNK + PIECE, PIECE, (bank_of(1, 5), bank_of(1, 6))),
        ]
        for a in range(PASSES):
            for half in halves:
                second_layer(CHUNK + half * PIECE, PIECE, [h10[half], h11[half]], last_banks[half], (a,))
